import numpy as np, ml_dtypes
CORES = [2,6,10,14,18,22,26,30]
N = 8
import mx_ref
BF = ml_dtypes.bfloat16
def entries(a):
    return np.ascontiguousarray(a.T).reshape(-1)
def table(e):
    return np.ascontiguousarray(np.reshape(e, (-1, 16)).T).astype(np.int32)
def tile(rs):
    return np.stack(rs, axis=2).reshape(128, -1).astype(BF)
def cut(t, i, w=512):
    return t[:, w * i:w * i + w]
def f(rng, *shape):
    return mx_ref.flush((rng.standard_normal(shape, dtype=np.float32) * np.exp2(rng.integers(-2, 3, shape[:-1] + (1,)))).astype(BF))
def wide(rng, *shape, cols=0):
    v = rng.standard_normal(shape, dtype=np.float32) * np.exp2(rng.integers(-12, 13, shape)).astype(np.float32)
    if cols: v *= np.repeat(np.exp2(rng.integers(-cols, cols + 1, shape[:-2] + (1, shape[-1] // 4))) * (rng.random(shape[:-2] + (1, shape[-1] // 4)) > 0.0625), 4, axis=-1).astype(np.float32)
    return mx_ref.flush(v.astype(BF))
T, CAPP, P = 512, 48, 256
SL = N * CAPP
G = 1
def pieces(rng, how):
    if how == "ones": n = np.ones((G, SL), int)
    elif how == "full":
        n = T - rng.integers(0, 8, (G, SL)); n[:, ::4] = T
    elif how == "powers":
        k = [1 << i for i in range(T.bit_length())]; k = sorted(set(k + [i + 1 for i in k if i < T]))
        n = rng.permuted(np.tile(np.resize(k, SL), (G, 1)), axis=1)
    else: n = np.where(rng.random((G, SL)) < 0.5, rng.integers(1, T + 1, (G, SL)), np.clip(np.exp2(rng.uniform(0, T.bit_length() - 1, (G, SL))).astype(int), 1, T))
    s = rng.integers(0, T - n + 1)
    if how == "full": s[:] = 0
    if how == "nested":
        for g in range(G):
            for r in range(N):
                m = rng.integers(0, T)
                b = np.sort(rng.choice(rng.integers(0, m + 1, 16), CAPP)); e = np.sort(rng.choice(rng.integers(m, T, 16), CAPP))[::-1]
                k = r * CAPP + rng.permutation(CAPP); s[g, k] = b; n[g, k] = e - b + 1
    return s, n
def lists(rng, how="any", every=False):
    held = np.zeros((N, N, CAPP), bool)
    for r in range(N):
        n = rng.integers(0, CAPP + 1, N); n[(r + rng.integers(1, N)) % N] = CAPP
        for q in range(N): held[q, r, rng.permutation(CAPP)[:CAPP if every else n[q]]] = True
    d = {"lo": [], "ln": [], "pf": [], "pg": []}
    for q in range(N):
        s, n = pieces(rng, how); e = ~held[q].reshape(-1)
        s[:, e] = -1; n[:, e] = 0
        d["lo"].append(table(s)); d["ln"].append(table(n))
    who = rng.permutation(N)
    for r in range(N):
        k = rng.permutation(np.flatnonzero(held[:, r]))
        first = rng.permutation(np.resize(k, P))
        second = np.where(rng.random(P) < 0.25, -1, rng.choice(k, P))
        if how == "ones":
            if r == who[0]:
                first[rng.permutation(P)[:P // 2]] = k[0]; second[rng.permutation(P)[:P // 2]] = k[0]
            if r == who[1]: second[:] = -1
            if r == who[2]: second = rng.choice(k, P)
        d["pf"].append(table(first))
        d["pg"].append(table(second))
    return {k: np.stack(t) for k, t in d.items()}
def setup_inputs(rng):
    return {"x": f(rng, N, 128, 4 * T), "a": f(rng, N, 128, 2048), "u": f(rng, N, 128, 512), "v": f(rng, N, 128, 512), **lists(rng)}
def setup_inputs_ones(rng):
    return {**setup_inputs(rng), **lists(rng, "ones")}
def setup_inputs_full(rng):
    return {**setup_inputs(rng), **lists(rng, "full", True)}
def setup_inputs_powers(rng):
    return {**setup_inputs(rng), **lists(rng, "powers", True)}
def setup_inputs_nested(rng):
    return {**setup_inputs(rng), **lists(rng, "nested", True)}
def setup_inputs_spread(rng):
    d = setup_inputs(rng); d["x"] = wide(rng, N, 128, 4 * T, cols=8); return d
def check_inputs(d):
    b = []; held = []
    for q in range(N):
        s, n = entries(d["lo"][q]).reshape(G, -1), entries(d["ln"][q]).reshape(G, -1)
        e = s == -1; held.append(~e[0])
        if s.min() < -1 or s.max() >= T or (e != e[:1]).any(): b.append("lo")
        if (n[e] != 0).any() or (n[~e] < 1).any() or (n[~e] > T - s[~e]).any(): b.append("ln")
    for r in range(N):
        h = np.concatenate([held[q][r * CAPP:r * CAPP + CAPP] for q in range(N)])
        for k, least in (("pf", 0), ("pg", -1)):
            j = entries(d[k][r])
            if j.min() < least or j.max() >= SL or not h[j[(j >= 0) & (j < SL)]].all(): b.append(k)
    return b
def reference(x, a, u, v, lo, ln, pf, pg):
    sent = []
    for q in range(N):
        X = mx_ref.quantize(x[q])
        Z = np.stack([mx_ref.matmul(mx_ref.quantize(np.ascontiguousarray(cut(a[q], i))), X) for i in range(4)])
        h = np.maximum(Z, np.float32(0)) * np.float32(0.05)
        s, n = entries(lo[q]), entries(ln[q])
        R = np.zeros((4, 128, SL), np.float32)
        for k in range(SL):
            if n[k]: R[:, :, k] = h[:, :, s[k]:s[k] + n[k]].max(axis=2)
        sent.append([mx_ref.quantize(np.ascontiguousarray(tile([R[i][:, CAPP * r:CAPP * r + CAPP] for i in range(4)]))) for r in range(N)])
    y = np.zeros((N, 128, P), np.float32)
    for r in range(N):
        V, U = mx_ref.quantize(v[r]), mx_ref.quantize(u[r])
        zv = np.concatenate([mx_ref.matmul(V, sent[q][r]) for q in range(N)], axis=1)
        zu = np.concatenate([mx_ref.matmul(U, sent[q][r]) for q in range(N)], axis=1)
        first, second = entries(pf[r]), entries(pg[r])
        y[r] = zv[:, first]
        two = second >= 0
        y[r][:, two] += zu[:, second[two]]
    return {"y": y}

@@ -1,0 +1,476 @@
+from concourse.bass import DstId, RemoteDMATransfer
+from concourse.mybir import dt, AluOpType, ActivationFunctionType
+
+N, CAPP, NT, P = 8, 48, 512, 256
+SL = N * CAPP
+LC = SL // 16
+HALF = SL // 2
+B1, B2 = 2, 5
+W1, W2 = 1 << B1, 1 << B2
+N1, N2 = NT // W1, NT // W2
+PER = W2 // W1
+O_S2, O_S1, O_H, O_P1, O_P2 = 0, NT, 2 * NT, 3 * NT, 4 * NT
+W = 5 * NT
+ND = 4 * N2
+AGAIN = ND + 8
+D2 = AGAIN + ND
+PH = 8 * D2
+D1 = PH + (PER - 3) * NT
+WR = D1 + NT
+ZERO = 8 * AGAIN + 7
+K1, K2, K8, K16 = 0, NT, 2 * NT, 3 * NT + PER
+KALL = K16 + D2 + N2
+TRI, PAIR = 0, 3 * HALF
+KG = 5 * HALF
+ZCOL = SL
+BY_V = (1, 2, 3)
+
+SCRATCH = {
+    "xs": ("sbuf", [128, 4 * NT], "bfloat16"),
+    "as_": ("sbuf", [128, 2048], "bfloat16"),
+    "us": ("sbuf", [128, 512], "bfloat16"),
+    "vs": ("sbuf", [128, 512], "bfloat16"),
+    "xq": ("sbuf", [128, NT], "float8_e4m3fn_x4"),
+    "xp": ("sbuf", [128, NT], "uint8"),
+    "aq": ("sbuf", [128, 512], "float8_e4m3fn_x4"),
+    "ap_": ("sbuf", [128, 512], "uint8"),
+    "uq": ("sbuf", [128, 128], "float8_e4m3fn_x4"),
+    "up": ("sbuf", [128, 128], "uint8"),
+    "vq": ("sbuf", [128, 128], "float8_e4m3fn_x4"),
+    "vp": ("sbuf", [128, 128], "uint8"),
+    "z": ("psum", [128, 4096], "float32"),
+    "win": ("sbuf", [128, 4 * W], "bfloat16"),
+    "runs": ("sbuf", [128, WR], "bfloat16"),
+    "d2": ("sbuf", [128, D2], "bfloat16"),
+    "mk": ("sbuf", [128, KALL], "bfloat16"),
+    "mg": ("sbuf", [128, KG], "bfloat16"),
+    "tile": ("sbuf", [128, 4 * SL], "bfloat16"),
+    "fq": ("sbuf", [128, HALF], "float8_e4m3fn_x4"),
+    "fp": ("sbuf", [128, HALF], "uint8"),
+    "nq": ("sbuf", [128, HALF], "float8_e4m3fn_x4"),
+    "np_": ("sbuf", [128, HALF], "uint8"),
+    "rfq": ("sbuf", [128, HALF], "float8_e4m3fn_x4"),
+    "rfp": ("sbuf", [128, HALF], "uint8"),
+    "rnq": ("sbuf", [128, HALF], "float8_e4m3fn_x4"),
+    "rnp": ("sbuf", [128, HALF], "uint8"),
+    "zv": ("sbuf", [128, SL], "float32"),
+    "zu": ("sbuf", [128, SL + 16], "float32"),
+    "gy": ("sbuf", [128, P], "float32"),
+    "ys": ("sbuf", [128, P], "float32"),
+    "offs": ("sbuf", [128, 2 * LC], "uint16"),
+    "offr": ("sbuf", [128, LC], "uint16"),
+    "offsl": ("sbuf", [128, 2 * LC], "uint16"),
+    "offrl": ("sbuf", [128, LC], "uint16"),
+    "l_x": ("sbuf", [128, 4 * LC], "int32"),
+    "lns": ("sbuf", [128, LC], "int32"),
+    "l_e": ("sbuf", [128, LC], "int32"),
+    "l_v1": ("sbuf", [128, 4 * LC], "int32"),
+    "l_v2": ("sbuf", [128, 4 * LC], "int32"),
+    "l_d": ("sbuf", [128, 4 * LC], "int32"),
+    "l_u": ("sbuf", [128, 4 * LC], "int32"),
+    "l_c": ("sbuf", [128, 2 * LC], "int32"),
+    "l_g": ("sbuf", [128, 4 * LC], "int32"),
+    "l_o": ("sbuf", [128, 2 * LC], "int32"),
+    "l_pm": ("sbuf", [128, LC], "int32"),
+    "l_hi": ("sbuf", [128, LC], "int32"),
+    "l_q8": ("sbuf", [128, LC], "int32"),
+    "l_pm5": ("sbuf", [128, LC], "int32"),
+    "l_hi5": ("sbuf", [128, LC], "int32"),
+    "l_f1": ("sbuf", [128, LC], "int32"),
+    "l_fp": ("sbuf", [128, 2 * LC], "int32"),
+    "l_m": ("sbuf", [128, 2 * LC], "int32"),
+    "l_r": ("sbuf", [128, LC], "int32"),
+    "pfs": ("sbuf", [128, P // 16], "int32"),
+    "pgs": ("sbuf", [128, P // 16], "int32"),
+    "pgt": ("sbuf", [128, P // 16], "int32"),
+    "pgn": ("sbuf", [128, P // 16], "int32"),
+    "pfo": ("sbuf", [128, P // 16], "uint16"),
+    "pgo": ("sbuf", [128, P // 16], "uint16"),
+}
+for _i in range(4):
+    _k = 2 if _i in BY_V else 3
+    SCRATCH["g%d" % _i] = ("sbuf", [128, _k * SL], "bfloat16")
+    SCRATCH["m%d" % _i] = ("sbuf", [128, _k * SL], "bfloat16")
+
+STEPS = ["t", "l1", "e", "r", "v1", "v2", "d1", "d2", "pm", "u", "hi", "c", "g", "o0", "o1", "q8", "pm5", "hi5", "f1",
+         "gp", "f", "p", "m", "sum", "pgt", "pgn"]
+
+SEMAPHORES = (["lst", "lx0", "lx1", "la0", "la1", "la2", "luv", "lpl", "rep", "repr_", "o1", "o2", "vm",
+               "qx0", "qx1", "qa0", "qa1", "qa2", "quv", "gi", "gm", "d1s", "d2s", "rs", "mmh",
+               "qf", "qn", "zero", "pl", "own", "arrf", "arrn", "loc", "mfv", "mfu", "mnv", "mnu", "zvs", "zus",
+               "gy0", "gy1", "y0", "y1", "yo", "tlf", "tln", "grf", "grn"]
+              + ["k_%s" % _n for _n in STEPS]
+              + ["%s%d" % (_n, _i) for _i in range(4)
+                 for _n in ("mm", "rl", "p1_", "p2_", "ss", "ge", "mef", "men")])
+
+ADD, SUB, MUL, MAX, MIN = AluOpType.add, AluOpType.subtract, AluOpType.mult, AluOpType.max, AluOpType.min
+GE, GT, LT, NEQ, EQ = AluOpType.is_ge, AluOpType.is_gt, AluOpType.is_lt, AluOpType.not_equal, AluOpType.is_equal
+SHR, AND = AluOpType.arith_shift_right, AluOpType.bitwise_and
+RELU, COPY = ActivationFunctionType.Relu, ActivationFunctionType.Copy
+
+
+def rev(t, lo, hi):
+    return t[:, hi - 1:(lo - 1 if lo > 0 else None):-1]
+
+
+def engine_plan(core, dests, topo):
+    off = [d for d in dests if topo.chip(d) != topo.chip(core)]
+    pool = topo.engines(core, off[0])
+    per = 1
+    while 2 * per * len(off) <= len(pool):
+        per *= 2
+    masks = {}
+    for k, d in enumerate(off):
+        masks[d] = pool[k * per:(k + 1) * per]
+    for d in dests:
+        if d not in masks:
+            masks[d] = [e for e in topo.engines(core, d) if e not in pool][:2]
+    return masks
+
+
+def rank_program(g, core, T, topo):
+    rank = T.rank_of(core)
+    if rank is None:
+        return
+    cores = T.cores
+    S = T.sem
+    v, s, te, sy = g.vector, g.scalar, g.tensor, g.sync
+
+    def group(c, far):
+        a = topo.chip(c)
+        return [q for q in range(N)
+                if (topo.chip(cores[q]) != a and not topo.mates(topo.chip(cores[q]), a)) == far]
+
+    far, near = group(core, True), group(core, False)
+    fs, ns = far[0] * CAPP, near[0] * CAPP
+    L, L2, L3, L4 = LC, 2 * LC, 3 * LC, 4 * LC
+    XH = NT // 2
+
+    s.dma_start(T.l_x[0:16, 0:L], T.lo[:, :]).then_inc(S.lst, 16)
+    sy.dma_start(T.lns[0:16, :], T.ln[:, :]).then_inc(S.lst, 16)
+    sy.dma_start(T.xs[:, 0:4 * XH], T.x[:, 0:4 * XH]).then_inc(S.lx0, 16)
+    s.dma_start(T.as_[:, 0:512], T.a[:, 0:512]).then_inc(S.la0, 16)
+    sy.dma_start(T.xs[:, 4 * XH:4 * NT], T.x[:, 4 * XH:4 * NT]).then_inc(S.lx1, 16)
+    sy.dma_start(T.as_[:, 512:1024], T.a[:, 512:1024]).then_inc(S.la1, 16)
+    sy.dma_start(T.as_[:, 1024:2048], T.a[:, 1024:2048]).then_inc(S.la2, 16)
+
+    g.iota(T.mg[:, :], [[0, KG]], 1, 0, allow_small_or_imprecise_dtypes=True).then_inc(S.gi, 1)
+    g.wait_ge(S.gi, 1)
+    for o, k in ((TRI, 3), (PAIR, 2)):
+        m = T.mg[:, o:o + k * HALF]
+        g.affine_select(m, m, [[0, HALF], [1, k]], NEQ, 0.0, 0, 0).then_inc(S.gm, 1)
+
+    v.memset(T.mk[:, :], 1.0).then_inc(S.vm, 1)
+    v.memset(T.runs[:, 8 * ND + 7:PH:8], 0.0).then_inc(S.rs, 1)
+    v.memset(T.d2[:, ND:AGAIN], 0.0).then_inc(S.zero, 1)
+    v.wait_ge(S.vm, 1)
+    for b, e, w in ((K1, K2, W1), (K2, K8, W2), (K8, K16, PER), (K16, KALL, N2)):
+        v.memset(T.mk[:, b:e:w], 0.0).then_inc(S.vm, 1)
+
+    def op(name, ins):
+        ins.then_inc(S["k_" + name], 1)
+
+    def need(*names):
+        for n in names:
+            v.wait_ge(S["k_" + n], 1)
+
+    def pa(t, a=None, b=None):
+        return t[0:16, :] if a is None else t[0:16, a:b]
+
+    v.wait_ge(S.lst, 32)
+    op("t", v.tensor_tensor(pa(T.l_x, L2, L3), pa(T.l_x, 0, L), pa(T.lns), ADD))
+    op("l1", v.tensor_scalar(pa(T.l_x, L, L2), pa(T.l_x, 0, L), -1.0, None, ADD))
+    need("t")
+    op("r", v.tensor_scalar(pa(T.l_x, L3, L4), pa(T.l_x, L2, L3), -1.0, None, ADD))
+    op("e", v.tensor_scalar(pa(T.l_e), pa(T.l_x, 0, L), float(O_H), None, ADD))
+    need("l1", "r")
+    op("v1", v.tensor_scalar(pa(T.l_v1), pa(T.l_x), B1, None, SHR))
+    op("v2", v.tensor_scalar(pa(T.l_v2), pa(T.l_x), B2, None, SHR))
+    need("v1")
+    op("d1", v.tensor_tensor(pa(T.l_d, 0, L2), pa(T.l_v1, L2, L4), pa(T.l_v1, 0, L2), SUB))
+    need("v2")
+    op("d2", v.tensor_tensor(pa(T.l_d, L2, L4), pa(T.l_v2, L2, L4), pa(T.l_v2, 0, L2), SUB))
+    op("pm", v.tensor_scalar(pa(T.l_pm), pa(T.l_v1, 0, L), PER - 1, None, AND))
+    need("d1", "d2")
+    op("u", v.tensor_scalar(pa(T.l_u), pa(T.l_d), 1.0, float(NT), MIN, MUL))
+    op("hi", v.tensor_scalar(pa(T.l_hi), pa(T.l_v2, 0, L), 3, None, SHR))
+    need("u")
+    op("c", v.tensor_tensor(pa(T.l_c), pa(T.l_u, 0, L2), pa(T.l_u, L2, L4), ADD))
+    op("g", v.tensor_scalar(pa(T.l_g, 0, L3), pa(T.l_d, 0, L3), 2.0, None, GE))
+    need("c", "e")
+    op("o0", v.tensor_tensor(pa(T.l_o, 0, L), pa(T.l_e), pa(T.l_c, 0, L), SUB))
+    op("o1", v.tensor_tensor(pa(T.l_o, L, L2), pa(T.l_x, L3, L4), pa(T.l_c, L, L2), ADD))
+    op("q8", v.tensor_scalar(pa(T.l_q8), pa(T.l_v2, L2, L3), 8.0, None, MUL))
+    need("o0", "o1")
+    v.tensor_copy(pa(T.offsl), pa(T.l_o)).then_inc(S.o1, 1)
+
+    def quant_a(lo, hi, load, q):
+        v.wait_ge(load, 16)
+        v.quantize_mx(T.aq[:, lo:hi], T.ap_[:, lo:hi], T.as_[:, 4 * lo:4 * hi]).then_inc(q, 1)
+
+    def quant_x(lo, hi, load, q):
+        v.wait_ge(load, 16)
+        v.quantize_mx(T.xq[:, lo:hi], T.xp[:, lo:hi], T.xs[:, 4 * lo:4 * hi]).then_inc(q, 1)
+
+    quant_x(0, XH, S.lx0, S.qx0)
+    quant_a(0, 128, S.la0, S.qa0)
+    quant_x(XH, NT, S.lx1, S.qx1)
+
+    need("hi", "q8")
+    op("hi5", v.tensor_scalar(pa(T.l_hi5), pa(T.l_hi), float(8 * AGAIN - 8), float(-8 - ZERO), MUL, ADD))
+    op("f1", v.tensor_tensor(pa(T.l_f1), pa(T.l_q8), pa(T.l_v2, 0, L), ADD))
+    need("pm")
+    op("pm5", v.tensor_scalar(pa(T.l_pm5), pa(T.l_pm), float(NT), float(PH - 1 - ZERO), MUL, ADD))
+    need("g")
+    op("gp", v.tensor_tensor(pa(T.l_g, L3, L4), pa(T.l_g, 0, L), pa(T.l_u, L2, L3), GT))
+    need("hi5", "f1")
+    op("f", v.tensor_tensor(pa(T.l_fp, 0, L), pa(T.l_f1), pa(T.l_hi5), ADD))
+    need("pm5")
+    op("p", v.tensor_tensor(pa(T.l_fp, L, L2), pa(T.l_v1, L2, L3), pa(T.l_pm5), ADD))
+    need("gp", "f", "p")
+    op("m", v.tensor_tensor(pa(T.l_m), pa(T.l_fp), pa(T.l_g, L2, L4), MUL))
+    quant_a(128, 256, S.la1, S.qa1)
+    need("m")
+    op("sum", v.tensor_tensor(pa(T.l_r), pa(T.l_m, 0, L), pa(T.l_m, L, L2), ADD))
+    need("sum")
+    v.tensor_scalar(pa(T.offrl), pa(T.l_r), float(ZERO), None, ADD).then_inc(S.o2, 1)
+
+    sy.wait_ge(S.o1, 1)
+    for k in range(8):
+        sy.dma_start(T.offs[16 * k:16 * k + 16, :], pa(T.offsl)).then_inc(S.rep, 16)
+    sy.wait_ge(S.o2, 1)
+    for k in range(8):
+        sy.dma_start(T.offr[16 * k:16 * k + 16, :], pa(T.offrl)).then_inc(S.repr_, 16)
+    sy.dma_start(T.vs[:, :], T.v[:, :]).then_inc(S.luv, 16)
+    sy.dma_start(T.us[:, :], T.u[:, :]).then_inc(S.luv, 16)
+    for k in range(8):
+        sy.dma_start(T.pfs[16 * k:16 * k + 16, :], T.pf[:, :]).then_inc(S.lpl, 16)
+        sy.dma_start(T.pgs[16 * k:16 * k + 16, :], T.pg[:, :]).then_inc(S.lpl, 16)
+
+    ZH = 2048
+
+    def product(out, n, i, c, sem):
+        te.matmul_mx(T.z[:, out:out + n], T.aq[:, 128 * i:128 * i + 128], T.ap_[:, 128 * i:128 * i + 128],
+                     T.xq[:, c:c + n], T.xp[:, c:c + n], True, True).then_inc(sem, 1)
+
+    te.wait_ge(S.qx0, 1)
+    te.wait_ge(S.qa0, 1)
+    product(ZH, XH, 0, 0, S.mmh)
+    te.wait_ge(S.qx1, 1)
+    product(0, XH, 0, XH, S.mm0)
+    te.wait_ge(S.qa1, 1)
+    product(512, NT, 1, 0, S.mm1)
+    te.wait_ge(S.qa2, 1)
+    product(1024, NT, 2, 0, S.mm2)
+    product(1536, NT, 3, 0, S.mm3)
+
+    def relu(i, frm, n, c, sem):
+        s.wait_ge(sem, 1)
+        h = i * W + O_H + c
+        s.activation(T.win[:, h:h + n], T.z[:, frm:frm + n], RELU, scale=0.05).then_inc(S["rl%d" % i], 1)
+
+    def per(i):
+        return 2 if i in BY_V else 3
+
+    def gather_p(i):
+        s.wait_ge(S["p1_%d" % i], 1)
+        s.wait_ge(S["p2_%d" % i], 1)
+        s.activation(T["g%d" % i][:, 1::per(i)], T.win[:, i * W + O_H:i * W + W].indirect(T.offs[:, L:L2]),
+                     COPY).then_inc(S["ge%d" % i], 1)
+
+    def gather_s(i):
+        s.wait_ge(S["ss%d" % i], 2)
+        s.activation(T["g%d" % i][:, 0::per(i)], T.win[:, i * W:i * W + O_P1].indirect(T.offs[:, 0:L]),
+                     COPY).then_inc(S["ge%d" % i], 1)
+
+    def runs(i, a):
+        return T.runs[:, i * N1:WR].indirect(T.offr[:, a // 16:(a + HALF) // 16])
+
+    relu(0, ZH, XH, 0, S.mmh)
+    relu(0, 0, XH, XH, S.mm0)
+    relu(1, 512, NT, 0, S.mm1)
+    s.wait_ge(S.rep, 128)
+    gather_p(0)
+    relu(2, 1024, NT, 0, S.mm2)
+    relu(3, 1536, NT, 0, S.mm3)
+    gather_s(0)
+    for i in (1, 2, 3):
+        gather_p(i)
+        gather_s(i)
+    n_runs = 1 + (PER - 3) + 8
+    s.wait_ge(S.rs, n_runs)
+    s.wait_ge(S.repr_, 128)
+    for a, sem in ((fs, S.grf), (ns, S.grn)):
+        s.activation(T.g0[:, 3 * a + 2:3 * (a + HALF):3], runs(0, a), COPY).then_inc(sem, 1)
+
+    def pick(d, first, b, w, n, sem):
+        g.affine_select(d[:, first:first + n], T.win[:, b + w - 1:b + NT:w], [[0, n]], EQ, 0.0, 0, 0).then_inc(sem, 1)
+
+    for i in range(4):
+        g.wait_ge(S["p1_%d" % i], 1)
+        pick(T.runs, D1 + i * N1, i * W + O_P1, W1, N1, S.d1s)
+        g.wait_ge(S["p2_%d" % i], 1)
+        for o in (0, AGAIN):
+            pick(T.d2, o + i * N2, i * W + O_P2, W2, N2, S.d2s)
+
+    def build_p(i):
+        w = i * W
+        v.wait_ge(S["rl%d" % i], 1 if i else 2)
+        for o, k, sem in ((O_P1, K1, "p1_%d"), (O_P2, K2, "p2_%d")):
+            v.tensor_tensor_scan(T.win[:, w + o:w + o + NT], T.mk[:, k:k + NT], T.win[:, w + O_H:w + O_H + NT], 0.0,
+                                 MUL, MAX).then_inc(S[sem % i], 1)
+
+    def build_s(i):
+        w = i * W
+        for o, k in ((O_S1, K1), (O_S2, K2)):
+            v.tensor_tensor_scan(rev(T.win, w + o, w + o + NT), T.mk[:, k:k + NT],
+                                 rev(T.win, w + O_H, w + O_H + NT), 0.0, MUL, MAX).then_inc(S["ss%d" % i], 1)
+
+    v.wait_ge(S.vm, 5)
+    build_p(0)
+    quant_a(256, 512, S.la2, S.qa2)
+    build_s(0)
+    for i in (1, 2, 3):
+        build_p(i)
+        build_s(i)
+    v.wait_ge(S.d1s, 4)
+    for m in range(PER - 3):
+        k, o = K8 + PER - 1 - m, PH + m * NT
+        v.tensor_tensor_scan(T.runs[:, o:o + NT], T.mk[:, k:k + NT], T.runs[:, D1:WR], 0.0, MUL, MAX).then_inc(S.rs, 1)
+    v.wait_ge(S.d2s, 8)
+    v.wait_ge(S.zero, 1)
+    for q in range(8):
+        k, n = K16 + N2 - 1 - q, D2 if q < 7 else ND
+        v.tensor_tensor_scan(T.runs[:, q:8 * n:8], T.mk[:, k:k + n], T.d2[:, 0:n], 0.0, MUL, MAX).then_inc(S.rs, 1)
+
+    def scan(i, a):
+        k = per(i)
+        m = (PAIR if k == 2 else TRI)
+        v.tensor_tensor_scan(T["m%d" % i][:, k * a:k * (a + HALF)], T.mg[:, m:m + k * HALF],
+                             T["g%d" % i][:, k * a:k * (a + HALF)], 0.0, MUL, MAX).then_inc(
+            S[("mef%d" if a == fs else "men%d") % i], 1)
+
+    def merged(i, a):
+        k = per(i)
+        M = T["m%d" % i][:, k * a + k - 1:k * (a + HALF):k]
+        dst = T.tile[:, 4 * a + i:4 * (a + HALF):4]
+        out = S.tlf if a == fs else S.tln
+        v.wait_ge(S[("mef%d" if a == fs else "men%d") % i], 1)
+        if k == 2:
+            v.tensor_tensor(dst, runs(i, a), M, MAX).then_inc(out, 1)
+        else:
+            v.tensor_copy(dst, M).then_inc(out, 1)
+
+    v.wait_ge(S.gm, 2)
+    for i in (1, 2):
+        v.wait_ge(S["ge%d" % i], 2)
+        scan(i, fs)
+        scan(i, ns)
+    v.wait_ge(S.rs, n_runs)
+    v.wait_ge(S.repr_, 128)
+    merged(1, fs)
+    merged(2, fs)
+    merged(1, ns)
+    v.wait_ge(S.ge3, 2)
+    scan(3, fs)
+    v.wait_ge(S.ge0, 2)
+    v.wait_ge(S.grf, 1)
+    scan(0, fs)
+    merged(3, fs)
+    merged(0, fs)
+    v.wait_ge(S.tlf, 4)
+    v.quantize_mx(T.fq[:, :], T.fp[:, :], T.tile[:, 4 * fs:4 * (fs + HALF)]).then_inc(S.qf, 1)
+    scan(3, ns)
+    merged(2, ns)
+    v.wait_ge(S.grn, 1)
+    scan(0, ns)
+    merged(3, ns)
+    merged(0, ns)
+    v.wait_ge(S.tln, 4)
+    v.quantize_mx(T.nq[:, :], T.np_[:, :], T.tile[:, 4 * ns:4 * (ns + HALF)]).then_inc(S.qn, 1)
+
+    n_loc = [0]
+
+    def send(isfar, mine, src_q, src_p, dst_q, dst_p, arr):
+        dests = [q for q in mine if q != rank]
+        masks = engine_plan(core, [cores[q] for q in dests], topo)
+        for codes in (True, False):
+            tr = []
+            for q in dests:
+                a = mine.index(q) * CAPP
+                b = group(cores[q], isfar).index(rank) * CAPP
+                rid, pid, _se = topo.addr(cores[q])
+                m = 0
+                for e in masks[cores[q]]:
+                    m |= 1 << e
+                    n_loc[0] += 1
+                if codes:
+                    src, dst = src_q[:, a:a + CAPP].bitcast(dt.uint8), dst_q[:, b:b + CAPP].bitcast(dt.uint8)
+                else:
+                    src, dst = src_p[:, a:a + CAPP], dst_p[:, b:b + CAPP]
+                tr.append(RemoteDMATransfer(dst_ids=[DstId(rid=rid, pnc=pid)], dma_engine_mask=m, remote_sem=arr,
+                                            src=src, dst=dst))
+            g.remote_dma_fused(tr, local_sem=S.loc)
+
+    def arrivals(isfar, mine):
+        n = 0
+        for q in mine:
+            if q != rank:
+                peers = [cores[p] for p in group(cores[q], isfar) if p != q]
+                n += 2 * len(engine_plan(cores[q], peers, topo)[core])
+        return n
+
+    g.wait_ge(S.qf, 1)
+    send(True, far, T.fq, T.fp, T.rfq, T.rfp, S.arrf)
+    g.wait_ge(S.qn, 1)
+    send(False, near, T.nq, T.np_, T.rnq, T.rnp, S.arrn)
+    g.wait_ge(S.loc, n_loc[0])
+
+    me = near.index(rank) * CAPP
+    sy.wait_ge(S.qn, 1)
+    sy.dma_start(T.rnq[:, me:me + CAPP].bitcast(dt.uint8), T.nq[:, me:me + CAPP].bitcast(dt.uint8)).then_inc(S.own, 16)
+    s.wait_ge(S.qn, 1)
+    s.dma_start(T.rnp[:, me:me + CAPP], T.np_[:, me:me + CAPP]).then_inc(S.own, 16)
+
+    v.wait_ge(S.luv, 32)
+    v.quantize_mx(T.vq[:, :], T.vp[:, :], T.vs[:, :]).then_inc(S.quv, 1)
+    v.quantize_mx(T.uq[:, :], T.up[:, :], T.us[:, :]).then_inc(S.quv, 1)
+    v.wait_ge(S.lpl, 256)
+    op("pgt", v.tensor_scalar(T.pgt[:, :], T.pgs[:, :], 0.0, float(ZCOL + 1), LT, MUL))
+    v.tensor_copy(T.pfo[:, :], T.pfs[:, :]).then_inc(S.pl, 1)
+    need("pgt")
+    op("pgn", v.tensor_tensor(T.pgn[:, :], T.pgs[:, :], T.pgt[:, :], ADD))
+    v.memset(T.zu[:, ZCOL:ZCOL + 16], 0.0).then_inc(S.zero, 1)
+    need("pgn")
+    v.tensor_copy(T.pgo[:, :], T.pgn[:, :]).then_inc(S.pl, 1)
+    v.wait_ge(S.zero, 2)
+
+    te.wait_ge(S.quv, 2)
+    for k, (arr, n, cq, cp, first, sv, su) in enumerate((
+            (S.arrf, arrivals(True, far), T.rfq, T.rfp, fs, S.mfv, S.mfu),
+            (S.arrn, arrivals(False, near), T.rnq, T.rnp, ns, S.mnv, S.mnu))):
+        bv, bu = 2048 + 1024 * k, 2560 + 1024 * k
+        te.wait_ge(arr, n)
+        if k:
+            te.wait_ge(S.own, 32)
+        te.matmul_mx(T.z[:, bv:bv + HALF], T.vq[:, :], T.vp[:, :], cq[:, :], cp[:, :], True, True).then_inc(sv, 1)
+        te.matmul_mx(T.z[:, bu:bu + HALF], T.uq[:, :], T.up[:, :], cq[:, :], cp[:, :], True, True).then_inc(su, 1)
+        s.wait_ge(sv, 1)
+        s.activation(T.zv[:, first:first + HALF], T.z[:, bv:bv + HALF], COPY).then_inc(S.zvs, 1)
+        v.wait_ge(su, 1)
+        v.tensor_copy(T.zu[:, first:first + HALF], T.z[:, bu:bu + HALF]).then_inc(S.zus, 1)
+
+    h, hc = P // 2, P // 32
+    s.wait_ge(S.pl, 2)
+    s.wait_ge(S.zvs, 2)
+    v.wait_ge(S.pl, 2)
+    v.wait_ge(S.zus, 2)
+    for k in range(2):
+        gy, yy = (S.gy0, S.gy1)[k], (S.y0, S.y1)[k]
+        s.activation(T.gy[:, k * h:k * h + h], T.zv[:, :].indirect(T.pfo[:, k * hc:k * hc + hc]), COPY).then_inc(gy, 1)
+        v.wait_ge(gy, 1)
+        v.tensor_tensor(T.ys[:, k * h:k * h + h], T.zu[:, :].indirect(T.pgo[:, k * hc:k * hc + hc]),
+                        T.gy[:, k * h:k * h + h], ADD).then_inc(yy, 1)
+        sy.wait_ge(yy, 1)
+        sy.dma_start(T.y[:, k * h:k * h + h], T.ys[:, k * h:k * h + h]).then_inc(S.yo, 16)
+    sy.wait_ge(S.yo, 32)

@@ -4,7 +4,8 @@ from concourse.mybir import dt, AluOpType, ActivationFunctionType
 N, CAPP, NT, P = 8, 48, 512, 256
 SL = N * CAPP
 LC = SL // 16
-HALF = SL // 2
+HALF = 192
+QMIN = 128
 B1, B2 = 2, 5
 W1, W2 = 1 << B1, 1 << B2
 N1, N2 = NT // W1, NT // W2
@@ -22,8 +23,14 @@ K1, K2, K8, K16 = 0, NT, 2 * NT, 3 * NT + PER
 KALL = K16 + D2 + N2
 TRI, PAIR = 0, 3 * HALF
 KG = 5 * HALF
-ZCOL = SL
-BY_V = (1, 2, 3)
+LEAD = 16
+PAD = QMIN - 2 * CAPP
+GROUPS = (("hop",), ("plane", "mate"), ("peer",), ("own",))
+MODES = ("SVVV",) * 4
+PRODUCTS = (("hop",), ("own",), ("plane", "mate"), ("peer",))
+DEDUP = True
+LP = 16
+HALVED = (0,)
 
 SCRATCH = {
     "xs": ("sbuf", [128, 4 * NT], "bfloat16"),
@@ -31,7 +38,7 @@ SCRATCH = {
     "us": ("sbuf", [128, 512], "bfloat16"),
     "vs": ("sbuf", [128, 512], "bfloat16"),
     "xq": ("sbuf", [128, NT], "float8_e4m3fn_x4"),
-    "xp": ("sbuf", [128, NT], "uint8"),
+    "xp": ("sbuf", [128, QMIN + NT], "uint8"),
     "aq": ("sbuf", [128, 512], "float8_e4m3fn_x4"),
     "ap_": ("sbuf", [128, 512], "uint8"),
     "uq": ("sbuf", [128, 128], "float8_e4m3fn_x4"),
@@ -39,93 +46,81 @@ SCRATCH = {
     "vq": ("sbuf", [128, 128], "float8_e4m3fn_x4"),
     "vp": ("sbuf", [128, 128], "uint8"),
     "z": ("psum", [128, 4096], "float32"),
-    "win": ("sbuf", [128, 4 * W], "bfloat16"),
+    "win": ("sbuf", [128, 4, W], "bfloat16"),
     "runs": ("sbuf", [128, WR], "bfloat16"),
     "d2": ("sbuf", [128, D2], "bfloat16"),
     "mk": ("sbuf", [128, KALL], "bfloat16"),
     "mg": ("sbuf", [128, KG], "bfloat16"),
-    "tile": ("sbuf", [128, 4 * SL], "bfloat16"),
-    "fq": ("sbuf", [128, HALF], "float8_e4m3fn_x4"),
-    "fp": ("sbuf", [128, HALF], "uint8"),
-    "nq": ("sbuf", [128, HALF], "float8_e4m3fn_x4"),
-    "np_": ("sbuf", [128, HALF], "uint8"),
-    "rfq": ("sbuf", [128, HALF], "float8_e4m3fn_x4"),
-    "rfp": ("sbuf", [128, HALF], "uint8"),
-    "rnq": ("sbuf", [128, HALF], "float8_e4m3fn_x4"),
-    "rnp": ("sbuf", [128, HALF], "uint8"),
-    "zv": ("sbuf", [128, SL], "float32"),
-    "zu": ("sbuf", [128, SL + 16], "float32"),
+    "tile": ("sbuf", [128, 4 * (PAD + SL + 16)], "bfloat16"),
+    "rfq": ("sbuf", [128, HALF + CAPP], "float8_e4m3fn_x4"),
+    "rfp": ("sbuf", [128, SL], "uint8"),
+    "rnq": ("sbuf", [128, QMIN + 2 * CAPP], "float8_e4m3fn_x4"),
+    "rnp": ("sbuf", [128, QMIN + 2 * CAPP], "uint8"),
+    "zv": ("sbuf", [128, LEAD + SL], "float32"),
+    "zu": ("sbuf", [128, LEAD + SL], "float32"),
     "gy": ("sbuf", [128, P], "float32"),
     "ys": ("sbuf", [128, P], "float32"),
     "offs": ("sbuf", [128, 2 * LC], "uint16"),
     "offr": ("sbuf", [128, LC], "uint16"),
-    "offsl": ("sbuf", [128, 2 * LC], "uint16"),
-    "offrl": ("sbuf", [128, LC], "uint16"),
-    "l_x": ("sbuf", [128, 4 * LC], "int32"),
+    "l_x": ("sbuf", [128, 4, LC], "int32"),
     "lns": ("sbuf", [128, LC], "int32"),
-    "l_e": ("sbuf", [128, LC], "int32"),
-    "l_v1": ("sbuf", [128, 4 * LC], "int32"),
-    "l_v2": ("sbuf", [128, 4 * LC], "int32"),
-    "l_d": ("sbuf", [128, 4 * LC], "int32"),
-    "l_u": ("sbuf", [128, 4 * LC], "int32"),
-    "l_c": ("sbuf", [128, 2 * LC], "int32"),
-    "l_g": ("sbuf", [128, 4 * LC], "int32"),
-    "l_o": ("sbuf", [128, 2 * LC], "int32"),
+    "l_v1": ("sbuf", [128, 4, LC], "int32"),
+    "l_v2": ("sbuf", [128, 4, LC], "int32"),
+    "l_d": ("sbuf", [128, 4, LC], "float32"),
+    "l_u": ("sbuf", [128, 4, LC], "float32"),
+    "l_c": ("sbuf", [128, 2, LC], "float32"),
+    "l_g": ("sbuf", [128, 4, LC], "float32"),
+    "l_o": ("sbuf", [128, 2, 2, 2, 2, 3], "float32"),
     "l_pm": ("sbuf", [128, LC], "int32"),
-    "l_hi": ("sbuf", [128, LC], "int32"),
-    "l_q8": ("sbuf", [128, LC], "int32"),
-    "l_pm5": ("sbuf", [128, LC], "int32"),
-    "l_hi5": ("sbuf", [128, LC], "int32"),
-    "l_f1": ("sbuf", [128, LC], "int32"),
-    "l_fp": ("sbuf", [128, 2 * LC], "int32"),
-    "l_m": ("sbuf", [128, 2 * LC], "int32"),
-    "l_r": ("sbuf", [128, LC], "int32"),
-    "pfs": ("sbuf", [128, P // 16], "int32"),
-    "pgs": ("sbuf", [128, P // 16], "int32"),
-    "pgt": ("sbuf", [128, P // 16], "int32"),
-    "pgn": ("sbuf", [128, P // 16], "int32"),
-    "pfo": ("sbuf", [128, P // 16], "uint16"),
-    "pgo": ("sbuf", [128, P // 16], "uint16"),
+    "l_q8": ("sbuf", [128, LC], "float32"),
+    "l_pm5": ("sbuf", [128, LC], "float32"),
+    "l_hi5": ("sbuf", [128, LC], "float32"),
+    "l_f1": ("sbuf", [128, LC], "float32"),
+    "l_fp": ("sbuf", [128, 2, LC], "float32"),
+    "l_m": ("sbuf", [128, 2, LC], "float32"),
+    "l_r": ("sbuf", [128, 1, 2, 2, 2, 3], "float32"),
+    "y_l": ("sbuf", [128, P // 8], "int32"),
+    "y_o": ("sbuf", [128, P // 8], "uint16"),
 }
 for _i in range(4):
-    _k = 2 if _i in BY_V else 3
-    SCRATCH["g%d" % _i] = ("sbuf", [128, _k * SL], "bfloat16")
-    SCRATCH["m%d" % _i] = ("sbuf", [128, _k * SL], "bfloat16")
+    SCRATCH["g%d" % _i] = ("sbuf", [128, 3 * SL], "bfloat16")
+    SCRATCH["m%d" % _i] = ("sbuf", [128, 3 * (PAD + SL + 16)], "bfloat16")
+for _i in range(5):
+    SCRATCH["cq%d" % _i] = ("sbuf", [128, HALF], "float8_e4m3fn_x4")
+    SCRATCH["cp%d" % _i] = ("sbuf", [128, HALF], "uint8")
 
-STEPS = ["t", "l1", "e", "r", "v1", "v2", "d1", "d2", "pm", "u", "hi", "c", "g", "o0", "o1", "q8", "pm5", "hi5", "f1",
-         "gp", "f", "p", "m", "sum", "pgt", "pgn"]
+STEPS = ["t", "r", "v1", "v2", "d1", "d2", "pm", "u", "c", "g", "o0", "o1", "q8", "pm5", "hi5", "f1",
+         "gp", "f", "p", "m", "sum", "ends", "runs"]
 
-SEMAPHORES = (["lst", "lx0", "lx1", "la0", "la1", "la2", "luv", "lpl", "rep", "repr_", "o1", "o2", "vm",
-               "qx0", "qx1", "qa0", "qa1", "qa2", "quv", "gi", "gm", "d1s", "d2s", "rs", "mmh",
-               "qf", "qn", "zero", "pl", "own", "arrf", "arrn", "loc", "mfv", "mfu", "mnv", "mnu", "zvs", "zus",
-               "gy0", "gy1", "y0", "y1", "yo", "tlf", "tln", "grf", "grn"]
+V_ORDER = ("z z z z t z z r z z v1 v2 pm d1 d2 hi5 q8 u pm5 f1 c a0 o0 o1 g p ends x0 f x1 gp a1 m a2 sum a3 runs "
+           "S00 S01 P00 P01 "
+           "S10 P10 S20 S30 P20 P30 ph tp").split()
+S_ORDER = "r0 r1 r2 r3 s0 p0 s1 p1 s2 s3 p2 p30 R00 p3+ R0+".split()
+M_ORDER = ["s10", "s20"]
+for _k in range(len(GROUPS)):
+    M_ORDER += [_n + str(_k) for _n in ("m1", "m2", "s3", "s0", "m3", "m0")]
+    M_ORDER += ["s1%d" % (_k + 1), "s2%d" % (_k + 1), "q%d" % _k] if _k + 1 < len(GROUPS) else ["yl", "q%d" % _k]
+M_ORDER.insert(M_ORDER.index("q%d" % (len(GROUPS) - 2)) + 1, "uv")
+
+SEMAPHORES = (["lst", "lx0", "lx1", "luv", "lpl", "rep", "repr_", "vm",
+               "qx0", "qx1", "quv", "gi", "gm", "d1s", "d2s", "rs", "tz",
+               "zero", "pl", "arrf", "arrn", "arrp", "loc", "zvs", "zus", "zu0", "gy0", "gy1", "y0", "y1", "yo", "qt",
+               "tl0", "tl1", "tl2", "tl3", "tl4"]
               + ["k_%s" % _n for _n in STEPS]
               + ["%s%d" % (_n, _i) for _i in range(4)
-                 for _n in ("mm", "rl", "p1_", "p2_", "ss", "ge", "mef", "men")])
+                 for _n in ("la", "qa", "mm", "rl", "s1_", "s2_", "pp", "ge", "gr", "mv", "mu", "me")])
 
 ADD, SUB, MUL, MAX, MIN = AluOpType.add, AluOpType.subtract, AluOpType.mult, AluOpType.max, AluOpType.min
 GE, GT, LT, NEQ, EQ = AluOpType.is_ge, AluOpType.is_gt, AluOpType.is_lt, AluOpType.not_equal, AluOpType.is_equal
 SHR, AND = AluOpType.arith_shift_right, AluOpType.bitwise_and
-RELU, COPY = ActivationFunctionType.Relu, ActivationFunctionType.Copy
+RELU, COPY, SIGN = ActivationFunctionType.Relu, ActivationFunctionType.Copy, ActivationFunctionType.Sign
 
 
-def rev(t, lo, hi):
-    return t[:, hi - 1:(lo - 1 if lo > 0 else None):-1]
-
-
-def engine_plan(core, dests, topo):
-    off = [d for d in dests if topo.chip(d) != topo.chip(core)]
-    pool = topo.engines(core, off[0])
-    per = 1
-    while 2 * per * len(off) <= len(pool):
-        per *= 2
-    masks = {}
-    for k, d in enumerate(off):
-        masks[d] = pool[k * per:(k + 1) * per]
-    for d in dests:
-        if d not in masks:
-            masks[d] = [e for e in topo.engines(core, d) if e not in pool][:2]
-    return masks
+def kind(a, b, topo):
+    a, b = topo.chip(a), topo.chip(b)
+    if a == b:
+        return "home"
+    return "mate" if topo.mates(a, b) else "plane" if topo.same_plane(a, b) else "hop"
 
 
 def rank_program(g, core, T, topo):
@@ -136,341 +131,397 @@ def rank_program(g, core, T, topo):
     S = T.sem
     v, s, te, sy = g.vector, g.scalar, g.tensor, g.sync
 
-    def group(c, far):
-        a = topo.chip(c)
-        return [q for q in range(N)
-                if (topo.chip(cores[q]) != a and not topo.mates(topo.chip(cores[q]), a)) == far]
+    def ranks(c, kinds):
+        return [q for q in range(N) if kind(c, cores[q], topo) in kinds]
 
-    far, near = group(core, True), group(core, False)
-    fs, ns = far[0] * CAPP, near[0] * CAPP
-    L, L2, L3, L4 = LC, 2 * LC, 3 * LC, 4 * LC
+    NG = len(GROUPS)
+    peer = [q for q in ranks(core, ("home",)) if q != rank][0]
+    flip = (N - 1) ^ rank
+    turn = tuple(slice(None, None, -1 if flip >> b & 1 else 1) for b in (2, 1, 0))
+    first, size = [], []
+    for k in GROUPS:
+        places = sorted(q ^ flip for q in {"peer": [peer], "own": [rank]}.get(k[0], ranks(core, k)))
+        assert places[-1] - places[0] == len(places) - 1
+        first.append(places[0] * CAPP)
+        size.append(len(places) * CAPP)
+    place = [PAD + a for a in first]
+    first[-1] -= 16
+    size[-1] += 16
+    L = LC
     XH = NT // 2
 
-    s.dma_start(T.l_x[0:16, 0:L], T.lo[:, :]).then_inc(S.lst, 16)
-    sy.dma_start(T.lns[0:16, :], T.ln[:, :]).then_inc(S.lst, 16)
-    sy.dma_start(T.xs[:, 0:4 * XH], T.x[:, 0:4 * XH]).then_inc(S.lx0, 16)
-    s.dma_start(T.as_[:, 0:512], T.a[:, 0:512]).then_inc(S.la0, 16)
-    sy.dma_start(T.xs[:, 4 * XH:4 * NT], T.x[:, 4 * XH:4 * NT]).then_inc(S.lx1, 16)
-    sy.dma_start(T.as_[:, 512:1024], T.a[:, 512:1024]).then_inc(S.la1, 16)
-    sy.dma_start(T.as_[:, 1024:2048], T.a[:, 1024:2048]).then_inc(S.la2, 16)
+    def window(k):
+        n = max(size[k], QMIN)
+        return place[k] + size[k] - n, n
 
-    g.iota(T.mg[:, :], [[0, KG]], 1, 0, allow_small_or_imprecise_dtypes=True).then_inc(S.gi, 1)
-    g.wait_ge(S.gi, 1)
-    for o, k in ((TRI, 3), (PAIR, 2)):
-        m = T.mg[:, o:o + k * HALF]
-        g.affine_select(m, m, [[0, HALF], [1, k]], NEQ, 0.0, 0, 0).then_inc(S.gm, 1)
+    def once(q):
+        seen = {}
+
+        def wait(name, n):
+            if seen.get(name, 0) < n or not DEDUP:
+                seen[name] = n
+                q.wait_ge(S[name], n)
+        return wait
+
+    vw, sw = once(v), once(s)
+
+    def load_a(q, i):
+        q.dma_start(T.as_[:, 512 * i:512 * i + 512], T.a[:, 512 * i:512 * i + 512]).then_inc(S["la%d" % i], 16)
+
+    for p in range(0, LP, 16):
+        s.dma_start(T.l_x[p:p + 16, 0, :], T.lo[:, :]).then_inc(S.lst, 16)
+        sy.dma_start(T.lns[p:p + 16, :], T.ln[:, :]).then_inc(S.lst, 16)
+    sy.dma_start(T.xs[:, 0:4 * XH], T.x[:, 0:4 * XH]).then_inc(S.lx0, 16)
+    load_a(s, 0)
+    sy.dma_start(T.xs[:, 4 * XH:4 * NT], T.x[:, 4 * XH:4 * NT]).then_inc(S.lx1, 16)
+    load_a(sy, 1)
+    load_a(sy, 2)
+    load_a(sy, 3)
+
+    tri = T.mg[:, TRI:PAIR]
+    g.iota(tri, [[0, HALF], [1, 3]], 0, 0, allow_small_or_imprecise_dtypes=True).then_inc(S.gi, 1)
+    g.iota(T.mg[:, PAIR:KG], [[0, HALF], [1, 2]], 0, 0, allow_small_or_imprecise_dtypes=True).then_inc(S.gm, 1)
+    nz = 4 * PAD
+    g.iota(T.tile[:, 0:nz], [[0, nz]], 0, 0, allow_small_or_imprecise_dtypes=True).then_inc(S.tz, 1)
+    s.wait_ge(S.gi, 1)
+    s.activation(tri, tri, SIGN).then_inc(S.gm, 1)
 
     v.memset(T.mk[:, :], 1.0).then_inc(S.vm, 1)
-    v.memset(T.runs[:, 8 * ND + 7:PH:8], 0.0).then_inc(S.rs, 1)
-    v.memset(T.d2[:, ND:AGAIN], 0.0).then_inc(S.zero, 1)
-    v.wait_ge(S.vm, 1)
-    for b, e, w in ((K1, K2, W1), (K2, K8, W2), (K8, K16, PER), (K16, KALL, N2)):
-        v.memset(T.mk[:, b:e:w], 0.0).then_inc(S.vm, 1)
+    zeros = [(T.mk[:, b:e:w], S.vm) for b, e, w in ((K1, K2, W1), (K2, K8, W2), (K8, K16, PER), (K16, KALL, N2))]
+    zeros += [(T.runs[:, 8 * ND + 7:PH:8], S.rs)] + [(t, S.zero) for t in (T.d2[:, ND:AGAIN], T.zv[:, 0:LEAD],
+                                                                           T.zu[:, 0:LEAD])]
 
     def op(name, ins):
         ins.then_inc(S["k_" + name], 1)
 
     def need(*names):
         for n in names:
-            v.wait_ge(S["k_" + n], 1)
+            vw("k_" + n, 1)
 
     def pa(t, a=None, b=None):
-        return t[0:16, :] if a is None else t[0:16, a:b]
+        return t[0:LP] if a is None else t[0:LP, a, :] if b is None else t[0:LP, a:b, :]
 
-    v.wait_ge(S.lst, 32)
-    op("t", v.tensor_tensor(pa(T.l_x, L2, L3), pa(T.l_x, 0, L), pa(T.lns), ADD))
-    op("l1", v.tensor_scalar(pa(T.l_x, L, L2), pa(T.l_x, 0, L), -1.0, None, ADD))
-    need("t")
-    op("r", v.tensor_scalar(pa(T.l_x, L3, L4), pa(T.l_x, L2, L3), -1.0, None, ADD))
-    op("e", v.tensor_scalar(pa(T.l_e), pa(T.l_x, 0, L), float(O_H), None, ADD))
-    need("l1", "r")
-    op("v1", v.tensor_scalar(pa(T.l_v1), pa(T.l_x), B1, None, SHR))
-    op("v2", v.tensor_scalar(pa(T.l_v2), pa(T.l_x), B2, None, SHR))
-    need("v1")
-    op("d1", v.tensor_tensor(pa(T.l_d, 0, L2), pa(T.l_v1, L2, L4), pa(T.l_v1, 0, L2), SUB))
-    need("v2")
-    op("d2", v.tensor_tensor(pa(T.l_d, L2, L4), pa(T.l_v2, L2, L4), pa(T.l_v2, 0, L2), SUB))
-    op("pm", v.tensor_scalar(pa(T.l_pm), pa(T.l_v1, 0, L), PER - 1, None, AND))
-    need("d1", "d2")
-    op("u", v.tensor_scalar(pa(T.l_u), pa(T.l_d), 1.0, float(NT), MIN, MUL))
-    op("hi", v.tensor_scalar(pa(T.l_hi), pa(T.l_v2, 0, L), 3, None, SHR))
-    need("u")
-    op("c", v.tensor_tensor(pa(T.l_c), pa(T.l_u, 0, L2), pa(T.l_u, L2, L4), ADD))
-    op("g", v.tensor_scalar(pa(T.l_g, 0, L3), pa(T.l_d, 0, L3), 2.0, None, GE))
-    need("c", "e")
-    op("o0", v.tensor_tensor(pa(T.l_o, 0, L), pa(T.l_e), pa(T.l_c, 0, L), SUB))
-    op("o1", v.tensor_tensor(pa(T.l_o, L, L2), pa(T.l_x, L3, L4), pa(T.l_c, L, L2), ADD))
-    op("q8", v.tensor_scalar(pa(T.l_q8), pa(T.l_v2, L2, L3), 8.0, None, MUL))
-    need("o0", "o1")
-    v.tensor_copy(pa(T.offsl), pa(T.l_o)).then_inc(S.o1, 1)
+    def turned(t, row):
+        return t[(slice(0, LP), row) + turn + (slice(None),)]
 
-    def quant_a(lo, hi, load, q):
-        v.wait_ge(load, 16)
-        v.quantize_mx(T.aq[:, lo:hi], T.ap_[:, lo:hi], T.as_[:, 4 * lo:4 * hi]).then_inc(q, 1)
+    def quant_a(i):
+        v.wait_ge(S["la%d" % i], 16)
+        c = 128 * i
+        v.quantize_mx(T.aq[:, c:c + 128], T.ap_[:, c:c + 128], T.as_[:, 4 * c:4 * c + 512]).then_inc(S["qa%d" % i], 1)
 
     def quant_x(lo, hi, load, q):
         v.wait_ge(load, 16)
-        v.quantize_mx(T.xq[:, lo:hi], T.xp[:, lo:hi], T.xs[:, 4 * lo:4 * hi]).then_inc(q, 1)
+        v.quantize_mx(T.xq[:, lo:hi], T.xp[:, QMIN + lo:QMIN + hi], T.xs[:, 4 * lo:4 * hi]).then_inc(q, 1)
 
-    quant_x(0, XH, S.lx0, S.qx0)
-    quant_a(0, 128, S.la0, S.qa0)
-    quant_x(XH, NT, S.lx1, S.qx1)
+    lists = {
+        "t": ((), lambda: v.tensor_tensor(pa(T.l_x, 2), pa(T.l_x, 0), pa(T.lns), ADD)),
+        "r": (("t",), lambda: v.tensor_scalar(T.l_x[0:LP, 1::2, :], T.l_x[0:LP, 0::2, :], -1.0, None, ADD)),
+        "v1": (("r",), lambda: v.tensor_scalar(pa(T.l_v1), pa(T.l_x), B1, None, SHR)),
+        "v2": (("r",), lambda: v.tensor_scalar(pa(T.l_v2), pa(T.l_x), B2, None, SHR)),
+        "d1": (("v1",), lambda: v.tensor_tensor(pa(T.l_d, 0, 2), pa(T.l_v1, 2, 4), pa(T.l_v1, 0, 2), SUB)),
+        "d2": (("v2",), lambda: v.tensor_tensor(pa(T.l_d, 2, 4), pa(T.l_v2, 2, 4), pa(T.l_v2, 0, 2), SUB)),
+        "u": (("d1", "d2"), lambda: v.tensor_scalar(pa(T.l_u), pa(T.l_d), 1.0, float(NT), MIN, MUL)),
+        "c": (("u",), lambda: v.tensor_tensor(pa(T.l_c), pa(T.l_u, 0, 2), pa(T.l_u, 2, 4), ADD)),
+        "o0": (("c",), lambda: v.tensor_tensor(turned(T.l_o, 0), pa(T.l_x, 0), pa(T.l_c, 0), SUB)),
+        "o1": (("c",), lambda: v.tensor_tensor(turned(T.l_o, 1), pa(T.l_x, 3), pa(T.l_c, 1), ADD)),
+        "ends": (("o0", "o1"), lambda: v.tensor_scalar(pa(T.offs), pa(T.l_o), float(O_H), None, ADD)),
+        "more": (("o0", "o1"), lambda: [v.tensor_scalar(T.offs[p:p + LP, :], pa(T.l_o), float(O_H), None, ADD).then_inc(
+            S.rep, 1) for p in range(LP, 128, LP)]),
+        "pm": (("v1",), lambda: v.tensor_scalar(pa(T.l_pm), pa(T.l_v1, 0), PER - 1, None, AND)),
+        "hi5": (("v2",), lambda: v.tensor_scalar(pa(T.l_hi5), pa(T.l_v2, 0), 8.0, float(8 * AGAIN - 8), GE, MUL)),
+        "g": (("d1", "d2"), lambda: v.tensor_scalar(pa(T.l_g, 0, 3), pa(T.l_d, 0, 3), 2.0, None, GE)),
+        "q8": (("v2",), lambda: v.tensor_scalar(pa(T.l_q8), pa(T.l_v2, 2), 8.0, float(-8 - ZERO), MUL, ADD)),
+        "pm5": (("pm",), lambda: v.tensor_scalar(pa(T.l_pm5), pa(T.l_pm), float(NT), float(PH - 1 - ZERO), MUL, ADD)),
+        "f1": (("q8",), lambda: v.tensor_tensor(pa(T.l_f1), pa(T.l_q8), pa(T.l_v2, 0), ADD)),
+        "gp": (("g", "u"), lambda: v.tensor_tensor(pa(T.l_g, 3), pa(T.l_g, 0), pa(T.l_u, 2), GT)),
+        "f": (("hi5", "f1"), lambda: v.tensor_tensor(pa(T.l_fp, 0), pa(T.l_f1), pa(T.l_hi5), ADD)),
+        "p": (("pm5",), lambda: v.tensor_tensor(pa(T.l_fp, 1), pa(T.l_v1, 2), pa(T.l_pm5), ADD)),
+        "m": (("gp", "f", "p"), lambda: v.tensor_tensor(pa(T.l_m), pa(T.l_fp), pa(T.l_g, 2, 4), MUL)),
+        "sum": (("m",), lambda: v.tensor_tensor(turned(T.l_r, 0), pa(T.l_m, 0), pa(T.l_m, 1), ADD)),
+        "runs": (("sum",), lambda: v.tensor_scalar(pa(T.offr), pa(T.l_r), float(ZERO), None, ADD)),
+    }
 
-    need("hi", "q8")
-    op("hi5", v.tensor_scalar(pa(T.l_hi5), pa(T.l_hi), float(8 * AGAIN - 8), float(-8 - ZERO), MUL, ADD))
-    op("f1", v.tensor_tensor(pa(T.l_f1), pa(T.l_q8), pa(T.l_v2, 0, L), ADD))
-    need("pm")
-    op("pm5", v.tensor_scalar(pa(T.l_pm5), pa(T.l_pm), float(NT), float(PH - 1 - ZERO), MUL, ADD))
-    need("g")
-    op("gp", v.tensor_tensor(pa(T.l_g, L3, L4), pa(T.l_g, 0, L), pa(T.l_u, L2, L3), GT))
-    need("hi5", "f1")
-    op("f", v.tensor_tensor(pa(T.l_fp, 0, L), pa(T.l_f1), pa(T.l_hi5), ADD))
-    need("pm5")
-    op("p", v.tensor_tensor(pa(T.l_fp, L, L2), pa(T.l_v1, L2, L3), pa(T.l_pm5), ADD))
-    need("gp", "f", "p")
-    op("m", v.tensor_tensor(pa(T.l_m), pa(T.l_fp), pa(T.l_g, L2, L4), MUL))
-    quant_a(128, 256, S.la1, S.qa1)
-    need("m")
-    op("sum", v.tensor_tensor(pa(T.l_r), pa(T.l_m, 0, L), pa(T.l_m, L, L2), ADD))
-    need("sum")
-    v.tensor_scalar(pa(T.offrl), pa(T.l_r), float(ZERO), None, ADD).then_inc(S.o2, 1)
-
-    sy.wait_ge(S.o1, 1)
-    for k in range(8):
-        sy.dma_start(T.offs[16 * k:16 * k + 16, :], pa(T.offsl)).then_inc(S.rep, 16)
-    sy.wait_ge(S.o2, 1)
-    for k in range(8):
-        sy.dma_start(T.offr[16 * k:16 * k + 16, :], pa(T.offrl)).then_inc(S.repr_, 16)
+    copies = 128 // LP - 1
+    for t, made, sem in ((T.offs, S.k_ends, S.rep), (T.offr, S.k_runs, S.repr_)):
+        if t is T.offs and "more" in V_ORDER:
+            continue
+        sy.wait_ge(made, 1)
+        for p in range(LP, 128, LP):
+            sy.dma_start(t[p:p + LP, :], pa(t)).then_inc(sem, 16)
     sy.dma_start(T.vs[:, :], T.v[:, :]).then_inc(S.luv, 16)
     sy.dma_start(T.us[:, :], T.u[:, :]).then_inc(S.luv, 16)
     for k in range(8):
-        sy.dma_start(T.pfs[16 * k:16 * k + 16, :], T.pf[:, :]).then_inc(S.lpl, 16)
-        sy.dma_start(T.pgs[16 * k:16 * k + 16, :], T.pg[:, :]).then_inc(S.lpl, 16)
+        sy.dma_start(T.y_l[16 * k:16 * k + 16, 0:P // 16], T.pf[:, :]).then_inc(S.lpl, 16)
+        sy.dma_start(T.y_l[16 * k:16 * k + 16, P // 16:P // 8], T.pg[:, :]).then_inc(S.lpl, 16)
 
-    ZH = 2048
+    def parts(i):
+        return ((0, XH), (XH, XH)) if i in HALVED else ((0, NT),)
 
-    def product(out, n, i, c, sem):
-        te.matmul_mx(T.z[:, out:out + n], T.aq[:, 128 * i:128 * i + 128], T.ap_[:, 128 * i:128 * i + 128],
-                     T.xq[:, c:c + n], T.xp[:, c:c + n], True, True).then_inc(sem, 1)
+    bank = {}
+    for i in range(4):
+        te.wait_ge(S["qa%d" % i], 1)
+        for c, n in parts(i):
+            if i == 0:
+                te.wait_ge(S.qx1 if c else S.qx0, 1)
+            b = bank[i, c] = 512 * len(bank)
+            te.matmul_mx(T.z[:, b:b + n], T.aq[:, 128 * i:128 * i + 128], T.ap_[:, 128 * i:128 * i + 128],
+                         T.xq[:, c:c + n], T.xp[:, QMIN + c:QMIN + c + n], True, True).then_inc(S["mm%d" % i], 1)
 
-    te.wait_ge(S.qx0, 1)
-    te.wait_ge(S.qa0, 1)
-    product(ZH, XH, 0, 0, S.mmh)
-    te.wait_ge(S.qx1, 1)
-    product(0, XH, 0, XH, S.mm0)
-    te.wait_ge(S.qa1, 1)
-    product(512, NT, 1, 0, S.mm1)
-    te.wait_ge(S.qa2, 1)
-    product(1024, NT, 2, 0, S.mm2)
-    product(1536, NT, 3, 0, S.mm3)
+    def relu(i):
+        for j, (c, n) in enumerate(parts(i)):
+            s.wait_ge(S["mm%d" % i], j + 1)
+            h, b = O_H + c, bank[i, c]
+            s.activation(T.win[:, i, h:h + n], T.z[:, b:b + n], RELU, scale=0.05).then_inc(S["rl%d" % i], 1)
 
-    def relu(i, frm, n, c, sem):
-        s.wait_ge(sem, 1)
-        h = i * W + O_H + c
-        s.activation(T.win[:, h:h + n], T.z[:, frm:frm + n], RELU, scale=0.05).then_inc(S["rl%d" % i], 1)
+    def per(i, k=0):
+        return 2 if MODES[k][i] in "VW" else 3
 
-    def per(i):
-        return 2 if i in BY_V else 3
+    def entry(i, e, a, n):
+        return T["g%d" % i][:, per(i) * a + e:per(i) * (a + n):per(i)]
 
-    def gather_p(i):
-        s.wait_ge(S["p1_%d" % i], 1)
-        s.wait_ge(S["p2_%d" % i], 1)
-        s.activation(T["g%d" % i][:, 1::per(i)], T.win[:, i * W + O_H:i * W + W].indirect(T.offs[:, L:L2]),
+    def gather_s(i, a=0, n=SL):
+        sw("s1_%d" % i, len(parts(i)))
+        sw("s2_%d" % i, len(parts(i)))
+        s.activation(entry(i, 0, a, n),
+                     T.win[:, i, 0:O_P1].indirect(T.offs[:, a // 16:(a + n) // 16]),
                      COPY).then_inc(S["ge%d" % i], 1)
 
-    def gather_s(i):
-        s.wait_ge(S["ss%d" % i], 2)
-        s.activation(T["g%d" % i][:, 0::per(i)], T.win[:, i * W:i * W + O_P1].indirect(T.offs[:, 0:L]),
+    def gather_p(i, a=0, n=SL):
+        sw("pp%d" % i, 2 * len(parts(i)))
+        s.activation(entry(i, 1, a, n),
+                     T.win[:, i, :].indirect(T.offs[:, L + a // 16:L + (a + n) // 16]),
                      COPY).then_inc(S["ge%d" % i], 1)
 
-    def runs(i, a):
-        return T.runs[:, i * N1:WR].indirect(T.offr[:, a // 16:(a + HALF) // 16])
+    def runs(i, a, n):
+        return T.runs[:, i * N1:WR].indirect(T.offr[:, a // 16:(a + n) // 16])
 
-    relu(0, ZH, XH, 0, S.mmh)
-    relu(0, 0, XH, XH, S.mm0)
-    relu(1, 512, NT, 0, S.mm1)
-    s.wait_ge(S.rep, 128)
-    gather_p(0)
-    relu(2, 1024, NT, 0, S.mm2)
-    relu(3, 1536, NT, 0, S.mm3)
-    gather_s(0)
-    for i in (1, 2, 3):
-        gather_p(i)
-        gather_s(i)
+    def who(k, modes):
+        return [i for i in range(4) if MODES[k][i] in modes]
+
+    def nth(order, name, key):
+        return sum(m.startswith(key) for m in order[:order.index(name) + 1])
+
+    def gather_runs(i, a, n):
+        sw("rs", n_runs)
+        sw("repr_", 16 * copies)
+        s.activation(entry(i, 2, a, n), runs(i, a, n), COPY).then_inc(S["ge%d" % i], 1)
+
+    def ends(i, k):
+        e, a, n = per(i, k), place[k], size[k]
+        return T.tile[:, 4 * place[k] + i:4 * (place[k] + n):4], T["m%d" % i][:, 3 * a + e - 1:3 * a + e * n:e]
+
+    def copy_s(i, k):
+        s.wait_ge(S["me%d" % i], nth(M_ORDER, "s%d%d" % (i, k), "s%d" % i))
+        dst, M = ends(i, k)
+        s.activation(dst, M, COPY).then_inc(S["tl%d" % k], 1)
+
     n_runs = 1 + (PER - 3) + 8
-    s.wait_ge(S.rs, n_runs)
-    s.wait_ge(S.repr_, 128)
-    for a, sem in ((fs, S.grf), (ns, S.grn)):
-        s.activation(T.g0[:, 3 * a + 2:3 * (a + HALF):3], runs(0, a), COPY).then_inc(sem, 1)
+    half = {"": (0, SL), "+": (first[1], SL - first[1]), "-": (first[2], SL - first[2])}
+    half.update({str(k): (first[k], size[k]) for k in range(NG)})
+    for name in S_ORDER:
+        if name == [m for m in S_ORDER if m[0] != "r"][0]:
+            s.wait_ge(S.k_ends, 1)
+            s.wait_ge(S.rep, copies if "more" in V_ORDER else 16 * copies)
+        i = int(name[1])
+        if name[0] == "r":
+            relu(i)
+        elif name[0] in "spR":
+            {"s": gather_s, "p": gather_p, "R": gather_runs}[name[0]](i, *half[name[2:]])
+        else:
+            copy_s(i, int(name[2]))
 
-    def pick(d, first, b, w, n, sem):
-        g.affine_select(d[:, first:first + n], T.win[:, b + w - 1:b + NT:w], [[0, n]], EQ, 0.0, 0, 0).then_inc(sem, 1)
+    def pick(out, in_, n, sem):
+        g.affine_select(out, in_, [[0, n]], EQ, 0.0, 0, 0).then_inc(sem, 1)
 
     for i in range(4):
-        g.wait_ge(S["p1_%d" % i], 1)
-        pick(T.runs, D1 + i * N1, i * W + O_P1, W1, N1, S.d1s)
-        g.wait_ge(S["p2_%d" % i], 1)
-        for o in (0, AGAIN):
-            pick(T.d2, o + i * N2, i * W + O_P2, W2, N2, S.d2s)
+        g.wait_ge(S["s1_%d" % i], len(parts(i)))
+        pick(T.runs[:, D1 + i * N1:D1 + i * N1 + N1], T.win[:, i, O_S1:O_S1 + NT:W1], N1, S.d1s)
+    for i in range(4):
+        g.wait_ge(S["s2_%d" % i], len(parts(i)))
+    for o in (0, AGAIN):
+        pick(T.d2[:, o:o + ND], T.win[:, :, O_S2:O_S2 + NT:W2], ND, S.d2s)
 
-    def build_p(i):
-        w = i * W
-        v.wait_ge(S["rl%d" % i], 1 if i else 2)
-        for o, k, sem in ((O_P1, K1, "p1_%d"), (O_P2, K2, "p2_%d")):
-            v.tensor_tensor_scan(T.win[:, w + o:w + o + NT], T.mk[:, k:k + NT], T.win[:, w + O_H:w + O_H + NT], 0.0,
-                                 MUL, MAX).then_inc(S[sem % i], 1)
+    def rev(i, lo, n):
+        return T.win[:, i, lo + n - 1:(lo - 1 if lo > 0 else None):-1]
 
-    def build_s(i):
-        w = i * W
-        for o, k in ((O_S1, K1), (O_S2, K2)):
-            v.tensor_tensor_scan(rev(T.win, w + o, w + o + NT), T.mk[:, k:k + NT],
-                                 rev(T.win, w + O_H, w + O_H + NT), 0.0, MUL, MAX).then_inc(S["ss%d" % i], 1)
+    def build(what, i, j):
+        c, n = parts(i)[j]
+        vw("vm", 5)
+        vw("rl%d" % i, j + 1)
+        for o, k, sem in ((O_S1, K1, "s1_%d"), (O_S2, K2, "s2_%d")) if what == "S" else ():
+            v.tensor_tensor_scan(rev(i, c + o, n), T.mk[:, k:k + n], rev(i, c + O_H, n), 0.0, MUL, MAX).then_inc(
+                S[sem % i], 1)
+        for o, k in ((O_P1, K1), (O_P2, K2)) if what == "P" else ():
+            v.tensor_tensor_scan(T.win[:, i, c + o:c + o + n], T.mk[:, k:k + n], T.win[:, i, c + O_H:c + O_H + n], 0.0,
+                                 MUL, MAX).then_inc(S["pp%d" % i], 1)
 
-    v.wait_ge(S.vm, 5)
-    build_p(0)
-    quant_a(256, 512, S.la2, S.qa2)
-    build_s(0)
-    for i in (1, 2, 3):
-        build_p(i)
-        build_s(i)
-    v.wait_ge(S.d1s, 4)
-    for m in range(PER - 3):
-        k, o = K8 + PER - 1 - m, PH + m * NT
-        v.tensor_tensor_scan(T.runs[:, o:o + NT], T.mk[:, k:k + NT], T.runs[:, D1:WR], 0.0, MUL, MAX).then_inc(S.rs, 1)
-    v.wait_ge(S.d2s, 8)
-    v.wait_ge(S.zero, 1)
-    for q in range(8):
-        k, n = K16 + N2 - 1 - q, D2 if q < 7 else ND
-        v.tensor_tensor_scan(T.runs[:, q:8 * n:8], T.mk[:, k:k + n], T.d2[:, 0:n], 0.0, MUL, MAX).then_inc(S.rs, 1)
+    def fine_runs():
+        v.wait_ge(S.d1s, 4)
+        for m in range(PER - 3):
+            k, o = K8 + PER - 1 - m, PH + m * NT
+            v.tensor_tensor_scan(T.runs[:, o:o + NT], T.mk[:, k:k + NT], T.runs[:, D1:WR], 0.0, MUL, MAX).then_inc(
+                S.rs, 1)
 
-    def scan(i, a):
-        k = per(i)
-        m = (PAIR if k == 2 else TRI)
-        v.tensor_tensor_scan(T["m%d" % i][:, k * a:k * (a + HALF)], T.mg[:, m:m + k * HALF],
-                             T["g%d" % i][:, k * a:k * (a + HALF)], 0.0, MUL, MAX).then_inc(
-            S[("mef%d" if a == fs else "men%d") % i], 1)
+    def coarse_runs():
+        v.wait_ge(S.d2s, 2)
+        v.wait_ge(S.zero, 3)
+        for q in range(8):
+            k, n = K16 + N2 - 1 - q, D2 if q < 7 else ND
+            v.tensor_tensor_scan(T.runs[:, q:8 * n:8], T.mk[:, k:k + n], T.d2[:, 0:n], 0.0, MUL, MAX).then_inc(S.rs, 1)
 
-    def merged(i, a):
-        k = per(i)
-        M = T["m%d" % i][:, k * a + k - 1:k * (a + HALF):k]
-        dst = T.tile[:, 4 * a + i:4 * (a + HALF):4]
-        out = S.tlf if a == fs else S.tln
-        v.wait_ge(S[("mef%d" if a == fs else "men%d") % i], 1)
-        if k == 2:
-            v.tensor_tensor(dst, runs(i, a), M, MAX).then_inc(out, 1)
+    for name in V_ORDER:
+        if name == "t":
+            v.wait_ge(S.lst, 2 * LP)
+        if name[0] == "z":
+            vw("vm", 1)
+            t, sem = zeros.pop(0)
+            v.memset(t, 0.0).then_inc(sem, 1)
+        elif name in lists:
+            need(*lists[name][0])
+            made = lists[name][1]()
+            if name != "more":
+                op(name, made)
+        elif name[0] == "x":
+            quant_x(*((XH, NT, S.lx1, S.qx1) if name == "x1" else (0, XH, S.lx0, S.qx0)))
+        elif name[0] == "a":
+            quant_a(int(name[1]))
+        elif name[0] in "SP":
+            build(name[0], int(name[1]), int(name[2]))
         else:
-            v.tensor_copy(dst, M).then_inc(out, 1)
+            (fine_runs if name == "PH".lower() else coarse_runs)()
+
+    def scan(i, k):
+        e, a, n = per(i, k), first[k], size[k]
+        m = (PAIR if e == 2 else TRI)
+        mine = [g_[2:] for g_ in S_ORDER if g_[0] in "spR" and g_[1] == str(i)]
+        vw("ge%d" % i, 1 + max(j for j, h in enumerate(mine) if h in ["", str(k)] + ["+", "-"][:k]))
+        if MODES[k][i] == "W":
+            vw("pp%d" % i, 2 * len(parts(i)))
+            v.tensor_tensor(ends(i, k)[1], T.win[:, i, :].indirect(T.offs[:, L + a // 16:L + (a + n) // 16]),
+                            entry(i, 0, a, n), MAX).then_inc(S["me%d" % i], 1)
+            return
+        v.tensor_tensor_scan(T["m%d" % i][:, 3 * place[k]:3 * place[k] + e * n], T.mg[:, m:m + e * n],
+                             T["g%d" % i][:, e * a:e * (a + n)], 0.0, MUL, MAX).then_inc(S["me%d" % i], 1)
+
+    def merged(i, k):
+        dst, M = ends(i, k)
+        v.wait_ge(S["me%d" % i], nth(M_ORDER, "s%d%d" % (i, k), "s%d" % i))
+        if per(i, k) == 2:
+            vw("rs", n_runs)
+            vw("repr_", 16 * copies)
+            v.tensor_tensor(dst, runs(i, first[k], size[k]), M, MAX).then_inc(S["tl%d" % k], 1)
+        else:
+            v.tensor_copy(dst, M).then_inc(S["tl%d" % k], 1)
+
+    def packed(k):
+        if k == 0:
+            return T.rnq, T.rnp
+        return T["cq%d" % k], T.xp if GROUPS[k] == ("peer",) else T["cp%d" % k]
+
+    def quant_tile(k):
+        c, n = window(k)
+        v.wait_ge(S["tl%d" % k], 4)
+        v.quantize_mx(packed(k)[0][:, 0:n], packed(k)[1][:, 0:n], T.tile[:, 4 * c:4 * (c + n)]).then_inc(S.qt, 1)
 
     v.wait_ge(S.gm, 2)
-    for i in (1, 2):
-        v.wait_ge(S["ge%d" % i], 2)
-        scan(i, fs)
-        scan(i, ns)
-    v.wait_ge(S.rs, n_runs)
-    v.wait_ge(S.repr_, 128)
-    merged(1, fs)
-    merged(2, fs)
-    merged(1, ns)
-    v.wait_ge(S.ge3, 2)
-    scan(3, fs)
-    v.wait_ge(S.ge0, 2)
-    v.wait_ge(S.grf, 1)
-    scan(0, fs)
-    merged(3, fs)
-    merged(0, fs)
-    v.wait_ge(S.tlf, 4)
-    v.quantize_mx(T.fq[:, :], T.fp[:, :], T.tile[:, 4 * fs:4 * (fs + HALF)]).then_inc(S.qf, 1)
-    scan(3, ns)
-    merged(2, ns)
-    v.wait_ge(S.grn, 1)
-    scan(0, ns)
-    merged(3, ns)
-    merged(0, ns)
-    v.wait_ge(S.tln, 4)
-    v.quantize_mx(T.nq[:, :], T.np_[:, :], T.tile[:, 4 * ns:4 * (ns + HALF)]).then_inc(S.qn, 1)
+    v.wait_ge(S.tz, 1)
+    for name in M_ORDER:
+        if name[0] in "sm":
+            (scan if name[0] == "s" else merged)(int(name[1]), int(name[2]))
+        elif name[0] == "q":
+            quant_tile(int(name[1]))
+        elif name == "yl":
+            v.wait_ge(S.lpl, 256)
+            v.tensor_scalar(T.y_o[:, :], T.y_l[:, :], float(LEAD), None, ADD).then_inc(S.pl, 1)
+        else:
+            v.wait_ge(S.luv, 32)
+            v.quantize_mx(T.vq[:, :], T.vp[:, :], T.vs[:, :]).then_inc(S.quv, 1)
+            v.quantize_mx(T.uq[:, :], T.up[:, :], T.us[:, :]).then_inc(S.quv, 1)
 
-    n_loc = [0]
+    def landing(q, c):
+        how = kind(c, cores[q], topo)
+        if how == "home":
+            return T.rfq, T.rfp, HALF, "arrp"
+        if how in GROUPS[0]:
+            return T.rnq, T.rnp, QMIN + ranks(c, GROUPS[0]).index(q) * CAPP, "arrn"
+        return T.rfq, T.rfp, ranks(c, GROUPS[1]).index(q) * CAPP, "arrf"
 
-    def send(isfar, mine, src_q, src_p, dst_q, dst_p, arr):
-        dests = [q for q in mine if q != rank]
-        masks = engine_plan(core, [cores[q] for q in dests], topo)
+    pool = topo.engines(core, cores[ranks(core, GROUPS[0])[0]])
+    rest = [e for e in topo.engines(core, cores[peer]) if e not in pool]
+
+    def transfer(k, q, codes, n, engines, skip=0):
+        a = PAD + (q ^ flip) * CAPP - window(k)[0] + skip
+        dq, dp, b, arr = landing(rank, cores[q])
+        b += skip
+        rid, pid, _se = topo.addr(cores[q])
+        if codes:
+            src, dst = packed(k)[0][:, a:a + n].bitcast(dt.uint8), dq[:, b:b + n].bitcast(dt.uint8)
+        else:
+            src, dst = packed(k)[1][:, a:a + n], dp[:, b:b + n]
+        count[arr] += len(engines)
+        return RemoteDMATransfer(dst_ids=[DstId(rid=rid, pnc=pid)], dma_engine_mask=sum(1 << e for e in engines),
+                                 remote_sem=S[arr], src=src, dst=dst)
+
+    count = {"arrf": 0, "arrn": 0, "arrp": 0}
+    for k in range(NG - 1):
+        g.wait_ge(S.qt, k + 1)
+        if GROUPS[k] == ("peer",):
+            g.remote_dma_fused([transfer(k, peer, True, CAPP, rest[0:2]),
+                                transfer(k, peer, False, 4 * CAPP, rest[2:4])], local_sem=S.loc)
+            continue
+        dests = ranks(core, GROUPS[k])
+        e = len(pool) // len(dests)
         for codes in (True, False):
-            tr = []
-            for q in dests:
-                a = mine.index(q) * CAPP
-                b = group(cores[q], isfar).index(rank) * CAPP
-                rid, pid, _se = topo.addr(cores[q])
-                m = 0
-                for e in masks[cores[q]]:
-                    m |= 1 << e
-                    n_loc[0] += 1
-                if codes:
-                    src, dst = src_q[:, a:a + CAPP].bitcast(dt.uint8), dst_q[:, b:b + CAPP].bitcast(dt.uint8)
-                else:
-                    src, dst = src_p[:, a:a + CAPP], dst_p[:, b:b + CAPP]
-                tr.append(RemoteDMATransfer(dst_ids=[DstId(rid=rid, pnc=pid)], dma_engine_mask=m, remote_sem=arr,
-                                            src=src, dst=dst))
+            tr = [transfer(k, q, codes, CAPP, pool[j * e:j * e + e]) for j, q in enumerate(dests)]
             g.remote_dma_fused(tr, local_sem=S.loc)
+    g.wait_ge(S.loc, sum(count.values()))
 
-    def arrivals(isfar, mine):
-        n = 0
-        for q in mine:
-            if q != rank:
-                peers = [cores[p] for p in group(cores[q], isfar) if p != q]
-                n += 2 * len(engine_plan(cores[q], peers, topo)[core])
-        return n
+    PL = P // 16
 
-    g.wait_ge(S.qf, 1)
-    send(True, far, T.fq, T.fp, T.rfq, T.rfp, S.arrf)
-    g.wait_ge(S.qn, 1)
-    send(False, near, T.nq, T.np_, T.rnq, T.rnp, S.arrn)
-    g.wait_ge(S.loc, n_loc[0])
-
-    me = near.index(rank) * CAPP
-    sy.wait_ge(S.qn, 1)
-    sy.dma_start(T.rnq[:, me:me + CAPP].bitcast(dt.uint8), T.nq[:, me:me + CAPP].bitcast(dt.uint8)).then_inc(S.own, 16)
-    s.wait_ge(S.qn, 1)
-    s.dma_start(T.rnp[:, me:me + CAPP], T.np_[:, me:me + CAPP]).then_inc(S.own, 16)
-
-    v.wait_ge(S.luv, 32)
-    v.quantize_mx(T.vq[:, :], T.vp[:, :], T.vs[:, :]).then_inc(S.quv, 1)
-    v.quantize_mx(T.uq[:, :], T.up[:, :], T.us[:, :]).then_inc(S.quv, 1)
-    v.wait_ge(S.lpl, 256)
-    op("pgt", v.tensor_scalar(T.pgt[:, :], T.pgs[:, :], 0.0, float(ZCOL + 1), LT, MUL))
-    v.tensor_copy(T.pfo[:, :], T.pfs[:, :]).then_inc(S.pl, 1)
-    need("pgt")
-    op("pgn", v.tensor_tensor(T.pgn[:, :], T.pgs[:, :], T.pgt[:, :], ADD))
-    v.memset(T.zu[:, ZCOL:ZCOL + 16], 0.0).then_inc(S.zero, 1)
-    need("pgn")
-    v.tensor_copy(T.pgo[:, :], T.pgn[:, :]).then_inc(S.pl, 1)
-    v.wait_ge(S.zero, 2)
-
+    count["qt"] = NG
+    parts_of = {
+        "own": ("qt",) + packed(NG - 1) + (QMIN - CAPP, CAPP, rank * CAPP)}
+    for how in ("hop", "plane", "mate", "peer"):
+        q = (ranks(core, (how,)) or [peer])[0]
+        dq, dp, b, arr = landing(q, core)
+        parts_of[how] = (arr, dq, dp, b, CAPP if q == peer else 2 * CAPP, q * CAPP)
     te.wait_ge(S.quv, 2)
-    for k, (arr, n, cq, cp, first, sv, su) in enumerate((
-            (S.arrf, arrivals(True, far), T.rfq, T.rfp, fs, S.mfv, S.mfu),
-            (S.arrn, arrivals(False, near), T.rnq, T.rnp, ns, S.mnv, S.mnu))):
-        bv, bu = 2048 + 1024 * k, 2560 + 1024 * k
-        te.wait_ge(arr, n)
-        if k:
-            te.wait_ge(S.own, 32)
-        te.matmul_mx(T.z[:, bv:bv + HALF], T.vq[:, :], T.vp[:, :], cq[:, :], cp[:, :], True, True).then_inc(sv, 1)
-        te.matmul_mx(T.z[:, bu:bu + HALF], T.uq[:, :], T.up[:, :], cq[:, :], cp[:, :], True, True).then_inc(su, 1)
-        s.wait_ge(sv, 1)
-        s.activation(T.zv[:, first:first + HALF], T.z[:, bv:bv + HALF], COPY).then_inc(S.zvs, 1)
-        v.wait_ge(su, 1)
-        v.tensor_copy(T.zu[:, first:first + HALF], T.z[:, bu:bu + HALF]).then_inc(S.zus, 1)
+    n_z = 0
+    for k, names in enumerate(PRODUCTS):
+        b0, b1 = 1024 * k, 1024 * k + 512
+        _w, cq, cp, _c, _n, _s = parts_of[names[0]]
+        hi = max(max(parts_of[m][3] + parts_of[m][4] for m in names), QMIN)
+        lo = min(min(parts_of[m][3] for m in names), hi - QMIN)
+        for m in names:
+            te.wait_ge(S[parts_of[m][0]], count[parts_of[m][0]])
+        for b, wq, wp, sem in ((b0, T.vq, T.vp, "mv%d"), (b1, T.uq, T.up, "mu%d")):
+            te.matmul_mx(T.z[:, b:b + hi - lo], wq[:, :], wp[:, :], cq[:, lo:hi], cp[:, lo:hi], True, True).then_inc(
+                S[sem % k], 1)
+        s.wait_ge(S["mv%d" % k], 1)
+        for m in names:
+            c, n, slot = parts_of[m][3:]
+            s.activation(T.zv[:, LEAD + slot:LEAD + slot + n], T.z[:, b0 + c - lo:b0 + c - lo + n], COPY).then_inc(
+                S.zvs, 1)
+        (v if k else s).wait_ge(S["mu%d" % k], 1)
+        for m in names:
+            c, n, slot = parts_of[m][3:]
+            dst, src = T.zu[:, LEAD + slot:LEAD + slot + n], T.z[:, b1 + c - lo:b1 + c - lo + n]
+            (v.tensor_copy(dst, src) if k else s.activation(dst, src, COPY)).then_inc(S.zus if k else S.zu0, 1)
+            n_z += 1
 
     h, hc = P // 2, P // 32
-    s.wait_ge(S.pl, 2)
-    s.wait_ge(S.zvs, 2)
-    v.wait_ge(S.pl, 2)
-    v.wait_ge(S.zus, 2)
+    s.wait_ge(S.pl, 1)
+    s.wait_ge(S.zvs, n_z)
+    v.wait_ge(S.pl, 1)
+    v.wait_ge(S.zus, n_z - 1)
+    v.wait_ge(S.zu0, 1)
     for k in range(2):
         gy, yy = (S.gy0, S.gy1)[k], (S.y0, S.y1)[k]
-        s.activation(T.gy[:, k * h:k * h + h], T.zv[:, :].indirect(T.pfo[:, k * hc:k * hc + hc]), COPY).then_inc(gy, 1)
+        s.activation(T.gy[:, k * h:k * h + h], T.zv[:, :].indirect(T.y_o[:, k * hc:k * hc + hc]), COPY).then_inc(gy, 1)
         v.wait_ge(gy, 1)
-        v.tensor_tensor(T.ys[:, k * h:k * h + h], T.zu[:, :].indirect(T.pgo[:, k * hc:k * hc + hc]),
+        v.tensor_tensor(T.ys[:, k * h:k * h + h], T.zu[:, :].indirect(T.y_o[:, PL + k * hc:PL + k * hc + hc]),
                         T.gy[:, k * h:k * h + h], ADD).then_inc(yy, 1)
-        sy.wait_ge(yy, 1)
-        sy.dma_start(T.y[:, k * h:k * h + h], T.ys[:, k * h:k * h + h]).then_inc(S.yo, 16)
+    for k, q in enumerate((sy, s)):
+        q.wait_ge((S.y0, S.y1)[k], 1)
+        q.dma_start(T.y[:, k * h:k * h + h], T.ys[:, k * h:k * h + h]).then_inc(S.yo, 16)
     sy.wait_ge(S.yo, 32)

@@ -92,15 +92,11 @@ for _i in range(5):
 STEPS = ["t", "r", "v1", "v2", "d1", "d2", "pm", "u", "c", "g", "o0", "o1", "q8", "pm5", "hi5", "f1",
          "gp", "f", "p", "m", "sum", "ends", "runs"]
 
-V_ORDER = ("z z z z t z z r z z v1 v2 pm d1 d2 hi5 q8 u pm5 f1 c a0 o0 o1 g p ends x0 f x1 gp a1 m a2 sum a3 runs "
-           "S00 S01 P00 P01 "
-           "S10 P10 S20 S30 P20 P30 ph tp").split()
-S_ORDER = "r0 r1 r2 r3 s0 p0 s1 p1 s2 s3 p2 p30 R00 p3+ R0+".split()
-M_ORDER = ["s10", "s20"]
-for _k in range(len(GROUPS)):
-    M_ORDER += [_n + str(_k) for _n in ("m1", "m2", "s3", "s0", "m3", "m0")]
-    M_ORDER += ["s1%d" % (_k + 1), "s2%d" % (_k + 1), "q%d" % _k] if _k + 1 < len(GROUPS) else ["yl", "q%d" % _k]
-M_ORDER.insert(M_ORDER.index("q%d" % (len(GROUPS) - 2)) + 1, "uv")
+V_ORDER = ("z z z z k k t k k r a0 v1 v2 x0 pm d1 d2 hi5 q8 x1 u pm5 f1 a1 c g p a2 o0 o1 a3 S100 ends S200 f P100 gp "
+           "P200 S101 S201 m P101 P201 sum S110 runs S210 P110 P210 S120 S220 S130 S230 P120 P220 P130 P230 "
+           "ph ph ph ph ph tp tp tp tp tp tp tp tp s10 s20 s30 m10 m20 s00 m30 s11 m00 s21 Q0 m11 m21 s31 s01 m31 m01 "
+           "s12 s22 s32 s02 Q1 m12 m22 m32 m02 s13 s23 s33 s03 Q2 V U m13 m23 m33 m03 yl Q3").split()
+S_ORDER = "r0 r1 r2 r3 s0 p0 s1 p1 s2 s30 p20 p30 R00 p2+ s3+ p3+ R0+".split()
 
 SEMAPHORES = (["lst", "lx0", "lx1", "luv", "lpl", "rep", "repr_", "vm",
                "qx0", "qx1", "quv", "gi", "gm", "d1s", "d2s", "rs", "tz",
@@ -287,6 +283,8 @@ def rank_program(g, core, T, topo):
                      COPY).then_inc(S["ge%d" % i], 1)
 
     def gather_p(i, a=0, n=SL):
+        sw("s1_%d" % i, len(parts(i)))
+        sw("s2_%d" % i, len(parts(i)))
         sw("pp%d" % i, 2 * len(parts(i)))
         s.activation(entry(i, 1, a, n),
                      T.win[:, i, :].indirect(T.offs[:, L + a // 16:L + (a + n) // 16]),
@@ -311,7 +309,7 @@ def rank_program(g, core, T, topo):
         return T.tile[:, 4 * place[k] + i:4 * (place[k] + n):4], T["m%d" % i][:, 3 * a + e - 1:3 * a + e * n:e]
 
     def copy_s(i, k):
-        s.wait_ge(S["me%d" % i], nth(M_ORDER, "s%d%d" % (i, k), "s%d" % i))
+        s.wait_ge(S["me%d" % i], nth(V_ORDER, "s%d%d" % (i, k), "s%d" % i))
         dst, M = ends(i, k)
         s.activation(dst, M, COPY).then_inc(S["tl%d" % k], 1)
 
@@ -344,53 +342,31 @@ def rank_program(g, core, T, topo):
     def rev(i, lo, n):
         return T.win[:, i, lo + n - 1:(lo - 1 if lo > 0 else None):-1]
 
-    def build(what, i, j):
+    def build(table, i, j):
         c, n = parts(i)[j]
         vw("vm", 5)
         vw("rl%d" % i, j + 1)
-        for o, k, sem in ((O_S1, K1, "s1_%d"), (O_S2, K2, "s2_%d")) if what == "S" else ():
-            v.tensor_tensor_scan(rev(i, c + o, n), T.mk[:, k:k + n], rev(i, c + O_H, n), 0.0, MUL, MAX).then_inc(
-                S[sem % i], 1)
-        for o, k in ((O_P1, K1), (O_P2, K2)) if what == "P" else ():
-            v.tensor_tensor_scan(T.win[:, i, c + o:c + o + n], T.mk[:, k:k + n], T.win[:, i, c + O_H:c + O_H + n], 0.0,
-                                 MUL, MAX).then_inc(S["pp%d" % i], 1)
-
-    def fine_runs():
-        v.wait_ge(S.d1s, 4)
-        for m in range(PER - 3):
-            k, o = K8 + PER - 1 - m, PH + m * NT
-            v.tensor_tensor_scan(T.runs[:, o:o + NT], T.mk[:, k:k + NT], T.runs[:, D1:WR], 0.0, MUL, MAX).then_inc(
-                S.rs, 1)
-
-    def coarse_runs():
-        v.wait_ge(S.d2s, 2)
-        v.wait_ge(S.zero, 3)
-        for q in range(8):
-            k, n = K16 + N2 - 1 - q, D2 if q < 7 else ND
-            v.tensor_tensor_scan(T.runs[:, q:8 * n:8], T.mk[:, k:k + n], T.d2[:, 0:n], 0.0, MUL, MAX).then_inc(S.rs, 1)
-
-    for name in V_ORDER:
-        if name == "t":
-            v.wait_ge(S.lst, 2 * LP)
-        if name[0] == "z":
-            vw("vm", 1)
-            t, sem = zeros.pop(0)
-            v.memset(t, 0.0).then_inc(sem, 1)
-        elif name in lists:
-            need(*lists[name][0])
-            made = lists[name][1]()
-            if name != "more":
-                op(name, made)
-        elif name[0] == "x":
-            quant_x(*((XH, NT, S.lx1, S.qx1) if name == "x1" else (0, XH, S.lx0, S.qx0)))
-        elif name[0] == "a":
-            quant_a(int(name[1]))
-        elif name[0] in "SP":
-            build(name[0], int(name[1]), int(name[2]))
+        o, k, sem = {"S1": (O_S1, K1, "s1_%d"), "S2": (O_S2, K2, "s2_%d"),
+                     "P1": (O_P1, K1, "pp%d"), "P2": (O_P2, K2, "pp%d")}[table]
+        if table[0] == "S":
+            out, h = rev(i, c + o, n), rev(i, c + O_H, n)
         else:
-            (fine_runs if name == "PH".lower() else coarse_runs)()
+            out, h = T.win[:, i, c + o:c + o + n], T.win[:, i, c + O_H:c + O_H + n]
+        v.tensor_tensor_scan(out, T.mk[:, k:k + n], h, 0.0, MUL, MAX).then_inc(S[sem % i], 1)
+
+    def fine_runs(m):
+        vw("d1s", 4)
+        k, o = K8 + PER - 1 - m, PH + m * NT
+        v.tensor_tensor_scan(T.runs[:, o:o + NT], T.mk[:, k:k + NT], T.runs[:, D1:WR], 0.0, MUL, MAX).then_inc(S.rs, 1)
+
+    def coarse_runs(q):
+        vw("d2s", 2)
+        vw("zero", 3)
+        k, n = K16 + N2 - 1 - q, D2 if q < 7 else ND
+        v.tensor_tensor_scan(T.runs[:, q:8 * n:8], T.mk[:, k:k + n], T.d2[:, 0:n], 0.0, MUL, MAX).then_inc(S.rs, 1)
 
     def scan(i, k):
+        vw("gm", 2)
         e, a, n = per(i, k), first[k], size[k]
         m = (PAIR if e == 2 else TRI)
         mine = [g_[2:] for g_ in S_ORDER if g_[0] in "spR" and g_[1] == str(i)]
@@ -405,7 +381,7 @@ def rank_program(g, core, T, topo):
 
     def merged(i, k):
         dst, M = ends(i, k)
-        v.wait_ge(S["me%d" % i], nth(M_ORDER, "s%d%d" % (i, k), "s%d" % i))
+        vw("me%d" % i, nth(V_ORDER, "s%d%d" % (i, k), "s%d" % i))
         if per(i, k) == 2:
             vw("rs", n_runs)
             vw("repr_", 16 * copies)
@@ -423,20 +399,38 @@ def rank_program(g, core, T, topo):
         v.wait_ge(S["tl%d" % k], 4)
         v.quantize_mx(packed(k)[0][:, 0:n], packed(k)[1][:, 0:n], T.tile[:, 4 * c:4 * (c + n)]).then_inc(S.qt, 1)
 
-    v.wait_ge(S.gm, 2)
-    v.wait_ge(S.tz, 1)
-    for name in M_ORDER:
-        if name[0] in "sm":
-            (scan if name[0] == "s" else merged)(int(name[1]), int(name[2]))
-        elif name[0] == "q":
+    assert [n for n in V_ORDER if n[0] == "Q"] == ["Q%d" % k for k in range(NG)]
+    for at, name in enumerate(V_ORDER):
+        seen = V_ORDER[:at].count(name)
+        if name in ("z", "k"):
+            if name == "k":
+                vw("vm", 1)
+            t, sem = zeros[seen + (4 if name == "z" else 0)]
+            v.memset(t, 0.0).then_inc(sem, 1)
+        elif name in lists:
+            vw("lst", 2 * LP)
+            need(*lists[name][0])
+            op(name, lists[name][1]())
+        elif name[0] == "x":
+            quant_x(*((XH, NT, S.lx1, S.qx1) if name == "x1" else (0, XH, S.lx0, S.qx0)))
+        elif name[0] == "a":
+            quant_a(int(name[1]))
+        elif name[0] in "SP":
+            build(name[:2], int(name[2]), int(name[3]))
+        elif name in ("ph", "tp"):
+            (fine_runs if name == "ph" else coarse_runs)(seen)
+        elif name[0] == "Q":
+            vw("tz", 1)
             quant_tile(int(name[1]))
         elif name == "yl":
             v.wait_ge(S.lpl, 256)
             v.tensor_scalar(T.y_o[:, :], T.y_l[:, :], float(LEAD), None, ADD).then_inc(S.pl, 1)
+        elif name in ("U", "V"):
+            vw("luv", 32)
+            q, p, t = (T.uq, T.up, T.us) if name == "U" else (T.vq, T.vp, T.vs)
+            v.quantize_mx(q[:, :], p[:, :], t[:, :]).then_inc(S.quv, 1)
         else:
-            v.wait_ge(S.luv, 32)
-            v.quantize_mx(T.vq[:, :], T.vp[:, :], T.vs[:, :]).then_inc(S.quv, 1)
-            v.quantize_mx(T.uq[:, :], T.up[:, :], T.us[:, :]).then_inc(S.quv, 1)
+            (scan if name[0] == "s" else merged)(int(name[1]), int(name[2]))
 
     def landing(q, c):
         how = kind(c, cores[q], topo)
@@ -466,8 +460,8 @@ def rank_program(g, core, T, topo):
     for k in range(NG - 1):
         g.wait_ge(S.qt, k + 1)
         if GROUPS[k] == ("peer",):
-            g.remote_dma_fused([transfer(k, peer, True, CAPP, rest[0:2]),
-                                transfer(k, peer, False, 4 * CAPP, rest[2:4])], local_sem=S.loc)
+            g.remote_dma_fused([transfer(k, peer, True, CAPP, rest[0:4]),
+                                transfer(k, peer, False, 4 * CAPP, rest[4:8])], local_sem=S.loc)
             continue
         dests = ranks(core, GROUPS[k])
         e = len(pool) // len(dests)

from concourse.bass import DstId, RemoteDMATransfer
from concourse.mybir import dt, AluOpType, ActivationFunctionType

N, CAPP, NT, P = 8, 48, 512, 256
SL = N * CAPP
LC = SL // 16
HALF = 192
QMIN = 128
B1, B2 = 2, 5
W1, W2 = 1 << B1, 1 << B2
N1, N2 = NT // W1, NT // W2
PER = W2 // W1
O_S2, O_S1, O_H, O_P1, O_P2 = 0, NT, 2 * NT, 3 * NT, 4 * NT
W = 5 * NT
ND = 4 * N2
AGAIN = ND + 8
D2 = AGAIN + ND
PH = 8 * D2
D1 = PH + (PER - 3) * NT
WR = D1 + NT
ZERO = 8 * AGAIN + 7
K1, K2, K8, K16 = 0, NT, 2 * NT, 3 * NT + PER
KALL = K16 + D2 + N2
TRI, PAIR = 0, 3 * HALF
KG = 5 * HALF
LEAD = 16
PAD = QMIN - 2 * CAPP
GROUPS = (("hop",), ("plane", "mate"), ("peer",), ("own",))
MODES = ("SVVV",) * 4
PRODUCTS = (("hop",), ("own",), ("plane", "mate"), ("peer",))
DEDUP = True
LP = 16
HALVED = (0,)

SCRATCH = {
    "xs": ("sbuf", [128, 4 * NT], "bfloat16"),
    "as_": ("sbuf", [128, 2048], "bfloat16"),
    "us": ("sbuf", [128, 512], "bfloat16"),
    "vs": ("sbuf", [128, 512], "bfloat16"),
    "xq": ("sbuf", [128, NT], "float8_e4m3fn_x4"),
    "xp": ("sbuf", [128, QMIN + NT], "uint8"),
    "aq": ("sbuf", [128, 512], "float8_e4m3fn_x4"),
    "ap_": ("sbuf", [128, 512], "uint8"),
    "uq": ("sbuf", [128, 128], "float8_e4m3fn_x4"),
    "up": ("sbuf", [128, 128], "uint8"),
    "vq": ("sbuf", [128, 128], "float8_e4m3fn_x4"),
    "vp": ("sbuf", [128, 128], "uint8"),
    "z": ("psum", [128, 4096], "float32"),
    "win": ("sbuf", [128, 4, W], "bfloat16"),
    "runs": ("sbuf", [128, WR], "bfloat16"),
    "d2": ("sbuf", [128, D2], "bfloat16"),
    "mk": ("sbuf", [128, KALL], "bfloat16"),
    "mg": ("sbuf", [128, KG], "bfloat16"),
    "tile": ("sbuf", [128, 4 * (PAD + SL + 16)], "bfloat16"),
    "rfq": ("sbuf", [128, HALF + CAPP], "float8_e4m3fn_x4"),
    "rfp": ("sbuf", [128, SL], "uint8"),
    "rnq": ("sbuf", [128, QMIN + 2 * CAPP], "float8_e4m3fn_x4"),
    "rnp": ("sbuf", [128, QMIN + 2 * CAPP], "uint8"),
    "zv": ("sbuf", [128, LEAD + SL], "float32"),
    "zu": ("sbuf", [128, LEAD + SL], "float32"),
    "gy": ("sbuf", [128, P], "float32"),
    "ys": ("sbuf", [128, P], "float32"),
    "offs": ("sbuf", [128, 2 * LC], "uint16"),
    "offr": ("sbuf", [128, LC], "uint16"),
    "l_x": ("sbuf", [128, 4, LC], "int32"),
    "lns": ("sbuf", [128, LC], "int32"),
    "l_v1": ("sbuf", [128, 4, LC], "int32"),
    "l_v2": ("sbuf", [128, 4, LC], "int32"),
    "l_d": ("sbuf", [128, 4, LC], "float32"),
    "l_u": ("sbuf", [128, 4, LC], "float32"),
    "l_c": ("sbuf", [128, 2, LC], "float32"),
    "l_g": ("sbuf", [128, 4, LC], "float32"),
    "l_o": ("sbuf", [128, 2, 2, 2, 2, 3], "float32"),
    "l_pm": ("sbuf", [128, LC], "int32"),
    "l_q8": ("sbuf", [128, LC], "float32"),
    "l_pm5": ("sbuf", [128, LC], "float32"),
    "l_hi5": ("sbuf", [128, LC], "float32"),
    "l_f1": ("sbuf", [128, LC], "float32"),
    "l_fp": ("sbuf", [128, 2, LC], "float32"),
    "l_m": ("sbuf", [128, 2, LC], "float32"),
    "l_r": ("sbuf", [128, 1, 2, 2, 2, 3], "float32"),
    "y_l": ("sbuf", [128, P // 8], "int32"),
    "y_o": ("sbuf", [128, P // 8], "uint16"),
}
for _i in range(4):
    SCRATCH["g%d" % _i] = ("sbuf", [128, 3 * SL], "bfloat16")
    SCRATCH["m%d" % _i] = ("sbuf", [128, 3 * (PAD + SL + 16)], "bfloat16")
for _i in range(5):
    SCRATCH["cq%d" % _i] = ("sbuf", [128, HALF], "float8_e4m3fn_x4")
    SCRATCH["cp%d" % _i] = ("sbuf", [128, HALF], "uint8")

STEPS = ["t", "r", "v1", "v2", "d1", "d2", "pm", "u", "c", "g", "o0", "o1", "q8", "pm5", "hi5", "f1",
         "gp", "f", "p", "m", "sum", "ends", "runs"]

V_ORDER = ("z z z z k k t k k r a0 v1 v2 x0 pm d1 d2 hi5 q8 x1 u pm5 f1 a1 c g p a2 o0 o1 a3 S100 ends S200 f P100 gp "
           "P200 S101 S201 m P101 P201 sum S110 runs S210 P110 P210 S120 S220 S130 S230 P120 P220 P130 P230 "
           "ph ph ph ph ph tp tp tp tp tp tp tp tp s10 s20 s30 m10 m20 s00 m30 s11 m00 s21 Q0 m11 m21 s31 s01 m31 m01 "
           "s12 s22 s32 s02 Q1 m12 m22 m32 m02 s13 s23 s33 s03 Q2 V U m13 m23 m33 m03 yl Q3").split()
S_ORDER = "r0 r1 r2 r3 s0 p0 s1 p1 s2 s30 p20 p30 R00 p2+ s3+ p3+ R0+".split()

SEMAPHORES = (["lst", "lx0", "lx1", "luv", "lpl", "rep", "repr_", "vm",
               "qx0", "qx1", "quv", "gi", "gm", "d1s", "d2s", "rs", "tz",
               "zero", "pl", "arrf", "arrn", "arrp", "loc", "zvs", "zus", "zu0", "gy0", "gy1", "y0", "y1", "yo", "qt",
               "tl0", "tl1", "tl2", "tl3", "tl4"]
              + ["k_%s" % _n for _n in STEPS]
              + ["%s%d" % (_n, _i) for _i in range(4)
                 for _n in ("la", "qa", "mm", "rl", "s1_", "s2_", "pp", "ge", "gr", "mv", "mu", "me")])

ADD, SUB, MUL, MAX, MIN = AluOpType.add, AluOpType.subtract, AluOpType.mult, AluOpType.max, AluOpType.min
GE, GT, LT, NEQ, EQ = AluOpType.is_ge, AluOpType.is_gt, AluOpType.is_lt, AluOpType.not_equal, AluOpType.is_equal
SHR, AND = AluOpType.arith_shift_right, AluOpType.bitwise_and
RELU, COPY, SIGN = ActivationFunctionType.Relu, ActivationFunctionType.Copy, ActivationFunctionType.Sign


def kind(a, b, topo):
    a, b = topo.chip(a), topo.chip(b)
    if a == b:
        return "home"
    return "mate" if topo.mates(a, b) else "plane" if topo.same_plane(a, b) else "hop"


def rank_program(g, core, T, topo):
    rank = T.rank_of(core)
    if rank is None:
        return
    cores = T.cores
    S = T.sem
    v, s, te, sy = g.vector, g.scalar, g.tensor, g.sync

    def ranks(c, kinds):
        return [q for q in range(N) if kind(c, cores[q], topo) in kinds]

    NG = len(GROUPS)
    peer = [q for q in ranks(core, ("home",)) if q != rank][0]
    flip = (N - 1) ^ rank
    turn = tuple(slice(None, None, -1 if flip >> b & 1 else 1) for b in (2, 1, 0))
    first, size = [], []
    for k in GROUPS:
        places = sorted(q ^ flip for q in {"peer": [peer], "own": [rank]}.get(k[0], ranks(core, k)))
        assert places[-1] - places[0] == len(places) - 1
        first.append(places[0] * CAPP)
        size.append(len(places) * CAPP)
    place = [PAD + a for a in first]
    first[-1] -= 16
    size[-1] += 16
    L = LC
    XH = NT // 2

    def window(k):
        n = max(size[k], QMIN)
        return place[k] + size[k] - n, n

    def once(q):
        seen = {}

        def wait(name, n):
            if seen.get(name, 0) < n or not DEDUP:
                seen[name] = n
                q.wait_ge(S[name], n)
        return wait

    vw, sw = once(v), once(s)

    def load_a(q, i):
        q.dma_start(T.as_[:, 512 * i:512 * i + 512], T.a[:, 512 * i:512 * i + 512]).then_inc(S["la%d" % i], 16)

    for p in range(0, LP, 16):
        s.dma_start(T.l_x[p:p + 16, 0, :], T.lo[:, :]).then_inc(S.lst, 16)
        sy.dma_start(T.lns[p:p + 16, :], T.ln[:, :]).then_inc(S.lst, 16)
    sy.dma_start(T.xs[:, 0:4 * XH], T.x[:, 0:4 * XH]).then_inc(S.lx0, 16)
    load_a(s, 0)
    sy.dma_start(T.xs[:, 4 * XH:4 * NT], T.x[:, 4 * XH:4 * NT]).then_inc(S.lx1, 16)
    load_a(sy, 1)
    load_a(sy, 2)
    load_a(sy, 3)

    tri = T.mg[:, TRI:PAIR]
    g.iota(tri, [[0, HALF], [1, 3]], 0, 0, allow_small_or_imprecise_dtypes=True).then_inc(S.gi, 1)
    g.iota(T.mg[:, PAIR:KG], [[0, HALF], [1, 2]], 0, 0, allow_small_or_imprecise_dtypes=True).then_inc(S.gm, 1)
    nz = 4 * PAD
    g.iota(T.tile[:, 0:nz], [[0, nz]], 0, 0, allow_small_or_imprecise_dtypes=True).then_inc(S.tz, 1)
    s.wait_ge(S.gi, 1)
    s.activation(tri, tri, SIGN).then_inc(S.gm, 1)

    v.memset(T.mk[:, :], 1.0).then_inc(S.vm, 1)
    zeros = [(T.mk[:, b:e:w], S.vm) for b, e, w in ((K1, K2, W1), (K2, K8, W2), (K8, K16, PER), (K16, KALL, N2))]
    zeros += [(T.runs[:, 8 * ND + 7:PH:8], S.rs)] + [(t, S.zero) for t in (T.d2[:, ND:AGAIN], T.zv[:, 0:LEAD],
                                                                           T.zu[:, 0:LEAD])]

    def op(name, ins):
        ins.then_inc(S["k_" + name], 1)

    def need(*names):
        for n in names:
            vw("k_" + n, 1)

    def pa(t, a=None, b=None):
        return t[0:LP] if a is None else t[0:LP, a, :] if b is None else t[0:LP, a:b, :]

    def turned(t, row):
        return t[(slice(0, LP), row) + turn + (slice(None),)]

    def quant_a(i):
        v.wait_ge(S["la%d" % i], 16)
        c = 128 * i
        v.quantize_mx(T.aq[:, c:c + 128], T.ap_[:, c:c + 128], T.as_[:, 4 * c:4 * c + 512]).then_inc(S["qa%d" % i], 1)

    def quant_x(lo, hi, load, q):
        v.wait_ge(load, 16)
        v.quantize_mx(T.xq[:, lo:hi], T.xp[:, QMIN + lo:QMIN + hi], T.xs[:, 4 * lo:4 * hi]).then_inc(q, 1)

    lists = {
        "t": ((), lambda: v.tensor_tensor(pa(T.l_x, 2), pa(T.l_x, 0), pa(T.lns), ADD)),
        "r": (("t",), lambda: v.tensor_scalar(T.l_x[0:LP, 1::2, :], T.l_x[0:LP, 0::2, :], -1.0, None, ADD)),
        "v1": (("r",), lambda: v.tensor_scalar(pa(T.l_v1), pa(T.l_x), B1, None, SHR)),
        "v2": (("r",), lambda: v.tensor_scalar(pa(T.l_v2), pa(T.l_x), B2, None, SHR)),
        "d1": (("v1",), lambda: v.tensor_tensor(pa(T.l_d, 0, 2), pa(T.l_v1, 2, 4), pa(T.l_v1, 0, 2), SUB)),
        "d2": (("v2",), lambda: v.tensor_tensor(pa(T.l_d, 2, 4), pa(T.l_v2, 2, 4), pa(T.l_v2, 0, 2), SUB)),
        "u": (("d1", "d2"), lambda: v.tensor_scalar(pa(T.l_u), pa(T.l_d), 1.0, float(NT), MIN, MUL)),
        "c": (("u",), lambda: v.tensor_tensor(pa(T.l_c), pa(T.l_u, 0, 2), pa(T.l_u, 2, 4), ADD)),
        "o0": (("c",), lambda: v.tensor_tensor(turned(T.l_o, 0), pa(T.l_x, 0), pa(T.l_c, 0), SUB)),
        "o1": (("c",), lambda: v.tensor_tensor(turned(T.l_o, 1), pa(T.l_x, 3), pa(T.l_c, 1), ADD)),
        "ends": (("o0", "o1"), lambda: v.tensor_scalar(pa(T.offs), pa(T.l_o), float(O_H), None, ADD)),
        "more": (("o0", "o1"), lambda: [v.tensor_scalar(T.offs[p:p + LP, :], pa(T.l_o), float(O_H), None, ADD).then_inc(
            S.rep, 1) for p in range(LP, 128, LP)]),
        "pm": (("v1",), lambda: v.tensor_scalar(pa(T.l_pm), pa(T.l_v1, 0), PER - 1, None, AND)),
        "hi5": (("v2",), lambda: v.tensor_scalar(pa(T.l_hi5), pa(T.l_v2, 0), 8.0, float(8 * AGAIN - 8), GE, MUL)),
        "g": (("d1", "d2"), lambda: v.tensor_scalar(pa(T.l_g, 0, 3), pa(T.l_d, 0, 3), 2.0, None, GE)),
        "q8": (("v2",), lambda: v.tensor_scalar(pa(T.l_q8), pa(T.l_v2, 2), 8.0, float(-8 - ZERO), MUL, ADD)),
        "pm5": (("pm",), lambda: v.tensor_scalar(pa(T.l_pm5), pa(T.l_pm), float(NT), float(PH - 1 - ZERO), MUL, ADD)),
        "f1": (("q8",), lambda: v.tensor_tensor(pa(T.l_f1), pa(T.l_q8), pa(T.l_v2, 0), ADD)),
        "gp": (("g", "u"), lambda: v.tensor_tensor(pa(T.l_g, 3), pa(T.l_g, 0), pa(T.l_u, 2), GT)),
        "f": (("hi5", "f1"), lambda: v.tensor_tensor(pa(T.l_fp, 0), pa(T.l_f1), pa(T.l_hi5), ADD)),
        "p": (("pm5",), lambda: v.tensor_tensor(pa(T.l_fp, 1), pa(T.l_v1, 2), pa(T.l_pm5), ADD)),
        "m": (("gp", "f", "p"), lambda: v.tensor_tensor(pa(T.l_m), pa(T.l_fp), pa(T.l_g, 2, 4), MUL)),
        "sum": (("m",), lambda: v.tensor_tensor(turned(T.l_r, 0), pa(T.l_m, 0), pa(T.l_m, 1), ADD)),
        "runs": (("sum",), lambda: v.tensor_scalar(pa(T.offr), pa(T.l_r), float(ZERO), None, ADD)),
    }

    copies = 128 // LP - 1
    for t, made, sem in ((T.offs, S.k_ends, S.rep), (T.offr, S.k_runs, S.repr_)):
        if t is T.offs and "more" in V_ORDER:
            continue
        sy.wait_ge(made, 1)
        for p in range(LP, 128, LP):
            sy.dma_start(t[p:p + LP, :], pa(t)).then_inc(sem, 16)
    sy.dma_start(T.vs[:, :], T.v[:, :]).then_inc(S.luv, 16)
    sy.dma_start(T.us[:, :], T.u[:, :]).then_inc(S.luv, 16)
    for k in range(8):
        sy.dma_start(T.y_l[16 * k:16 * k + 16, 0:P // 16], T.pf[:, :]).then_inc(S.lpl, 16)
        sy.dma_start(T.y_l[16 * k:16 * k + 16, P // 16:P // 8], T.pg[:, :]).then_inc(S.lpl, 16)

    def parts(i):
        return ((0, XH), (XH, XH)) if i in HALVED else ((0, NT),)

    bank = {}
    for i in range(4):
        te.wait_ge(S["qa%d" % i], 1)
        for c, n in parts(i):
            if i == 0:
                te.wait_ge(S.qx1 if c else S.qx0, 1)
            b = bank[i, c] = 512 * len(bank)
            te.matmul_mx(T.z[:, b:b + n], T.aq[:, 128 * i:128 * i + 128], T.ap_[:, 128 * i:128 * i + 128],
                         T.xq[:, c:c + n], T.xp[:, QMIN + c:QMIN + c + n], True, True).then_inc(S["mm%d" % i], 1)

    def relu(i):
        for j, (c, n) in enumerate(parts(i)):
            s.wait_ge(S["mm%d" % i], j + 1)
            h, b = O_H + c, bank[i, c]
            s.activation(T.win[:, i, h:h + n], T.z[:, b:b + n], RELU, scale=0.05).then_inc(S["rl%d" % i], 1)

    def per(i, k=0):
        return 2 if MODES[k][i] in "VW" else 3

    def entry(i, e, a, n):
        return T["g%d" % i][:, per(i) * a + e:per(i) * (a + n):per(i)]

    def gather_s(i, a=0, n=SL):
        sw("s1_%d" % i, len(parts(i)))
        sw("s2_%d" % i, len(parts(i)))
        s.activation(entry(i, 0, a, n),
                     T.win[:, i, 0:O_P1].indirect(T.offs[:, a // 16:(a + n) // 16]),
                     COPY).then_inc(S["ge%d" % i], 1)

    def gather_p(i, a=0, n=SL):
        sw("s1_%d" % i, len(parts(i)))
        sw("s2_%d" % i, len(parts(i)))
        sw("pp%d" % i, 2 * len(parts(i)))
        s.activation(entry(i, 1, a, n),
                     T.win[:, i, :].indirect(T.offs[:, L + a // 16:L + (a + n) // 16]),
                     COPY).then_inc(S["ge%d" % i], 1)

    def runs(i, a, n):
        return T.runs[:, i * N1:WR].indirect(T.offr[:, a // 16:(a + n) // 16])

    def who(k, modes):
        return [i for i in range(4) if MODES[k][i] in modes]

    def nth(order, name, key):
        return sum(m.startswith(key) for m in order[:order.index(name) + 1])

    def gather_runs(i, a, n):
        sw("rs", n_runs)
        sw("repr_", 16 * copies)
        s.activation(entry(i, 2, a, n), runs(i, a, n), COPY).then_inc(S["ge%d" % i], 1)

    def ends(i, k):
        e, a, n = per(i, k), place[k], size[k]
        return T.tile[:, 4 * place[k] + i:4 * (place[k] + n):4], T["m%d" % i][:, 3 * a + e - 1:3 * a + e * n:e]

    def copy_s(i, k):
        s.wait_ge(S["me%d" % i], nth(V_ORDER, "s%d%d" % (i, k), "s%d" % i))
        dst, M = ends(i, k)
        s.activation(dst, M, COPY).then_inc(S["tl%d" % k], 1)

    n_runs = 1 + (PER - 3) + 8
    half = {"": (0, SL), "+": (first[1], SL - first[1]), "-": (first[2], SL - first[2])}
    half.update({str(k): (first[k], size[k]) for k in range(NG)})
    for name in S_ORDER:
        if name == [m for m in S_ORDER if m[0] != "r"][0]:
            s.wait_ge(S.k_ends, 1)
            s.wait_ge(S.rep, copies if "more" in V_ORDER else 16 * copies)
        i = int(name[1])
        if name[0] == "r":
            relu(i)
        elif name[0] in "spR":
            {"s": gather_s, "p": gather_p, "R": gather_runs}[name[0]](i, *half[name[2:]])
        else:
            copy_s(i, int(name[2]))

    def pick(out, in_, n, sem):
        g.affine_select(out, in_, [[0, n]], EQ, 0.0, 0, 0).then_inc(sem, 1)

    for i in range(4):
        g.wait_ge(S["s1_%d" % i], len(parts(i)))
        pick(T.runs[:, D1 + i * N1:D1 + i * N1 + N1], T.win[:, i, O_S1:O_S1 + NT:W1], N1, S.d1s)
    for i in range(4):
        g.wait_ge(S["s2_%d" % i], len(parts(i)))
    for o in (0, AGAIN):
        pick(T.d2[:, o:o + ND], T.win[:, :, O_S2:O_S2 + NT:W2], ND, S.d2s)

    def rev(i, lo, n):
        return T.win[:, i, lo + n - 1:(lo - 1 if lo > 0 else None):-1]

    def build(table, i, j):
        c, n = parts(i)[j]
        vw("vm", 5)
        vw("rl%d" % i, j + 1)
        o, k, sem = {"S1": (O_S1, K1, "s1_%d"), "S2": (O_S2, K2, "s2_%d"),
                     "P1": (O_P1, K1, "pp%d"), "P2": (O_P2, K2, "pp%d")}[table]
        if table[0] == "S":
            out, h = rev(i, c + o, n), rev(i, c + O_H, n)
        else:
            out, h = T.win[:, i, c + o:c + o + n], T.win[:, i, c + O_H:c + O_H + n]
        v.tensor_tensor_scan(out, T.mk[:, k:k + n], h, 0.0, MUL, MAX).then_inc(S[sem % i], 1)

    def fine_runs(m):
        vw("d1s", 4)
        k, o = K8 + PER - 1 - m, PH + m * NT
        v.tensor_tensor_scan(T.runs[:, o:o + NT], T.mk[:, k:k + NT], T.runs[:, D1:WR], 0.0, MUL, MAX).then_inc(S.rs, 1)

    def coarse_runs(q):
        vw("d2s", 2)
        vw("zero", 3)
        k, n = K16 + N2 - 1 - q, D2 if q < 7 else ND
        v.tensor_tensor_scan(T.runs[:, q:8 * n:8], T.mk[:, k:k + n], T.d2[:, 0:n], 0.0, MUL, MAX).then_inc(S.rs, 1)

    def scan(i, k):
        vw("gm", 2)
        e, a, n = per(i, k), first[k], size[k]
        m = (PAIR if e == 2 else TRI)
        mine = [g_[2:] for g_ in S_ORDER if g_[0] in "spR" and g_[1] == str(i)]
        vw("ge%d" % i, 1 + max(j for j, h in enumerate(mine) if h in ["", str(k)] + ["+", "-"][:k]))
        if MODES[k][i] == "W":
            vw("pp%d" % i, 2 * len(parts(i)))
            v.tensor_tensor(ends(i, k)[1], T.win[:, i, :].indirect(T.offs[:, L + a // 16:L + (a + n) // 16]),
                            entry(i, 0, a, n), MAX).then_inc(S["me%d" % i], 1)
            return
        v.tensor_tensor_scan(T["m%d" % i][:, 3 * place[k]:3 * place[k] + e * n], T.mg[:, m:m + e * n],
                             T["g%d" % i][:, e * a:e * (a + n)], 0.0, MUL, MAX).then_inc(S["me%d" % i], 1)

    def merged(i, k):
        dst, M = ends(i, k)
        vw("me%d" % i, nth(V_ORDER, "s%d%d" % (i, k), "s%d" % i))
        if per(i, k) == 2:
            vw("rs", n_runs)
            vw("repr_", 16 * copies)
            v.tensor_tensor(dst, runs(i, first[k], size[k]), M, MAX).then_inc(S["tl%d" % k], 1)
        else:
            v.tensor_copy(dst, M).then_inc(S["tl%d" % k], 1)

    def packed(k):
        if k == 0:
            return T.rnq, T.rnp
        return T["cq%d" % k], T.xp if GROUPS[k] == ("peer",) else T["cp%d" % k]

    def quant_tile(k):
        c, n = window(k)
        v.wait_ge(S["tl%d" % k], 4)
        v.quantize_mx(packed(k)[0][:, 0:n], packed(k)[1][:, 0:n], T.tile[:, 4 * c:4 * (c + n)]).then_inc(S.qt, 1)

    assert [n for n in V_ORDER if n[0] == "Q"] == ["Q%d" % k for k in range(NG)]
    for at, name in enumerate(V_ORDER):
        seen = V_ORDER[:at].count(name)
        if name in ("z", "k"):
            if name == "k":
                vw("vm", 1)
            t, sem = zeros[seen + (4 if name == "z" else 0)]
            v.memset(t, 0.0).then_inc(sem, 1)
        elif name in lists:
            vw("lst", 2 * LP)
            need(*lists[name][0])
            op(name, lists[name][1]())
        elif name[0] == "x":
            quant_x(*((XH, NT, S.lx1, S.qx1) if name == "x1" else (0, XH, S.lx0, S.qx0)))
        elif name[0] == "a":
            quant_a(int(name[1]))
        elif name[0] in "SP":
            build(name[:2], int(name[2]), int(name[3]))
        elif name in ("ph", "tp"):
            (fine_runs if name == "ph" else coarse_runs)(seen)
        elif name[0] == "Q":
            vw("tz", 1)
            quant_tile(int(name[1]))
        elif name == "yl":
            v.wait_ge(S.lpl, 256)
            v.tensor_scalar(T.y_o[:, :], T.y_l[:, :], float(LEAD), None, ADD).then_inc(S.pl, 1)
        elif name in ("U", "V"):
            vw("luv", 32)
            q, p, t = (T.uq, T.up, T.us) if name == "U" else (T.vq, T.vp, T.vs)
            v.quantize_mx(q[:, :], p[:, :], t[:, :]).then_inc(S.quv, 1)
        else:
            (scan if name[0] == "s" else merged)(int(name[1]), int(name[2]))

    def landing(q, c):
        how = kind(c, cores[q], topo)
        if how == "home":
            return T.rfq, T.rfp, HALF, "arrp"
        if how in GROUPS[0]:
            return T.rnq, T.rnp, QMIN + ranks(c, GROUPS[0]).index(q) * CAPP, "arrn"
        return T.rfq, T.rfp, ranks(c, GROUPS[1]).index(q) * CAPP, "arrf"

    pool = topo.engines(core, cores[ranks(core, GROUPS[0])[0]])
    rest = [e for e in topo.engines(core, cores[peer]) if e not in pool]

    def transfer(k, q, codes, n, engines, skip=0):
        a = PAD + (q ^ flip) * CAPP - window(k)[0] + skip
        dq, dp, b, arr = landing(rank, cores[q])
        b += skip
        rid, pid, _se = topo.addr(cores[q])
        if codes:
            src, dst = packed(k)[0][:, a:a + n].bitcast(dt.uint8), dq[:, b:b + n].bitcast(dt.uint8)
        else:
            src, dst = packed(k)[1][:, a:a + n], dp[:, b:b + n]
        count[arr] += len(engines)
        return RemoteDMATransfer(dst_ids=[DstId(rid=rid, pnc=pid)], dma_engine_mask=sum(1 << e for e in engines),
                                 remote_sem=S[arr], src=src, dst=dst)

    count = {"arrf": 0, "arrn": 0, "arrp": 0}
    for k in range(NG - 1):
        g.wait_ge(S.qt, k + 1)
        if GROUPS[k] == ("peer",):
            g.remote_dma_fused([transfer(k, peer, True, CAPP, rest[0:4]),
                                transfer(k, peer, False, 4 * CAPP, rest[4:8])], local_sem=S.loc)
            continue
        dests = ranks(core, GROUPS[k])
        e = len(pool) // len(dests)
        for codes in (True, False):
            tr = [transfer(k, q, codes, CAPP, pool[j * e:j * e + e]) for j, q in enumerate(dests)]
            g.remote_dma_fused(tr, local_sem=S.loc)
    g.wait_ge(S.loc, sum(count.values()))

    PL = P // 16

    count["qt"] = NG
    parts_of = {
        "own": ("qt",) + packed(NG - 1) + (QMIN - CAPP, CAPP, rank * CAPP)}
    for how in ("hop", "plane", "mate", "peer"):
        q = (ranks(core, (how,)) or [peer])[0]
        dq, dp, b, arr = landing(q, core)
        parts_of[how] = (arr, dq, dp, b, CAPP if q == peer else 2 * CAPP, q * CAPP)
    te.wait_ge(S.quv, 2)
    n_z = 0
    for k, names in enumerate(PRODUCTS):
        b0, b1 = 1024 * k, 1024 * k + 512
        _w, cq, cp, _c, _n, _s = parts_of[names[0]]
        hi = max(max(parts_of[m][3] + parts_of[m][4] for m in names), QMIN)
        lo = min(min(parts_of[m][3] for m in names), hi - QMIN)
        for m in names:
            te.wait_ge(S[parts_of[m][0]], count[parts_of[m][0]])
        for b, wq, wp, sem in ((b0, T.vq, T.vp, "mv%d"), (b1, T.uq, T.up, "mu%d")):
            te.matmul_mx(T.z[:, b:b + hi - lo], wq[:, :], wp[:, :], cq[:, lo:hi], cp[:, lo:hi], True, True).then_inc(
                S[sem % k], 1)
        s.wait_ge(S["mv%d" % k], 1)
        for m in names:
            c, n, slot = parts_of[m][3:]
            s.activation(T.zv[:, LEAD + slot:LEAD + slot + n], T.z[:, b0 + c - lo:b0 + c - lo + n], COPY).then_inc(
                S.zvs, 1)
        (v if k else s).wait_ge(S["mu%d" % k], 1)
        for m in names:
            c, n, slot = parts_of[m][3:]
            dst, src = T.zu[:, LEAD + slot:LEAD + slot + n], T.z[:, b1 + c - lo:b1 + c - lo + n]
            (v.tensor_copy(dst, src) if k else s.activation(dst, src, COPY)).then_inc(S.zus if k else S.zu0, 1)
            n_z += 1

    h, hc = P // 2, P // 32
    s.wait_ge(S.pl, 1)
    s.wait_ge(S.zvs, n_z)
    v.wait_ge(S.pl, 1)
    v.wait_ge(S.zus, n_z - 1)
    v.wait_ge(S.zu0, 1)
    for k in range(2):
        gy, yy = (S.gy0, S.gy1)[k], (S.y0, S.y1)[k]
        s.activation(T.gy[:, k * h:k * h + h], T.zv[:, :].indirect(T.y_o[:, k * hc:k * hc + hc]), COPY).then_inc(gy, 1)
        v.wait_ge(gy, 1)
        v.tensor_tensor(T.ys[:, k * h:k * h + h], T.zu[:, :].indirect(T.y_o[:, PL + k * hc:PL + k * hc + hc]),
                        T.gy[:, k * h:k * h + h], ADD).then_inc(yy, 1)
    for k, q in enumerate((sy, s)):
        q.wait_ge((S.y0, S.y1)[k], 1)
        q.dma_start(T.y[:, k * h:k * h + h], T.ys[:, k * h:k * h + h]).then_inc(S.yo, 16)
    sy.wait_ge(S.yo, 32)
